import numpy as np
import ml_dtypes


def mxq(x, axis, fmt="e4m3"):
    dtype, down = {"e4m3": (ml_dtypes.float8_e4m3fn, 7), "e5m2": (ml_dtypes.float8_e5m2, 14)}[fmt]
    v = np.moveaxis(np.asarray(x, np.float32).astype(ml_dtypes.bfloat16).astype(np.float64), axis, -1)
    blocks = v.reshape(v.shape[:-1] + (-1, 32))
    amax = np.abs(blocks).max(-1, keepdims=True)
    byte = np.maximum(np.where(amax > 0, np.frexp(amax)[1] - 1 + 127, 0) - down, 1)
    scale = np.exp2(byte - 127.0)
    codes = (blocks / scale).astype(np.float32).astype(dtype).astype(np.float64)
    return np.moveaxis((codes * scale).reshape(v.shape), -1, axis)


WIDE = False


def mx_kscale(k):
    if not WIDE:
        return np.ones(k)
    levels = np.array([10, -10, 5, -5, 0])
    if k % 512:
        return np.exp2(np.random.permutation(np.resize(levels, k // 32))).repeat(32)
    a = np.empty((k // 512, 16))
    for p in range(k // 512):
        a[p, :8] = np.random.permutation(np.resize(levels, 8))
        for g in range(8):
            far = levels[np.abs(levels - a[p, g]) >= 10]
            a[p, g + 8] = far[np.random.randint(len(far))]
    return np.exp2(a.ravel()).repeat(32)


def f64(x):
    return np.asarray(x).astype(np.float64)


def striped(idx):
    return np.tile(idx.reshape(-1, 16).T, (8, 1)).astype(np.uint16)


def unstriped(offs):
    return offs[:16].T.reshape(-1).astype(np.int64)


E2M1 = np.array([0.0, 0.5, 1.0, 1.5, 2.0, 3.0, 4.0, 6.0, -0.0, -0.5, -1.0, -1.5, -2.0, -3.0, -4.0, -6.0])


def pack_weight(w, fmt):
    k, n = w.shape
    w = f64(np.asarray(w, np.float32).astype(ml_dtypes.bfloat16)).reshape(k // 32, 32, n)
    amax = np.abs(w).max(1)
    if fmt == "e4m3":
        byte = np.frexp(amax)[1] - 1 + 127 - 7
    else:
        mant, ex = np.frexp(amax / 6.0)
        byte = np.where(mant > 0.5, ex, ex - 1) + 127
    byte = np.clip(np.where(amax > 0, byte, 1), 1, 254)
    scaled = (w * np.exp2(127.0 - byte)[:, None, :]).reshape(k, n).astype(np.float32)
    by_word = np.ascontiguousarray(scaled.reshape(k // 512, 128, 4, n).transpose(0, 1, 3, 2))
    if fmt == "e4m3":
        words = by_word.astype(ml_dtypes.float8_e4m3fn).view(np.uint8)
    else:
        c = by_word.astype(ml_dtypes.float4_e2m1fn).view(np.uint8) & 0xF
        words = (c[..., 0::2] | (c[..., 1::2] << 4)).reshape(k // 512, 128, 2 * n)
    return np.ascontiguousarray(words), np.ascontiguousarray(byte.astype(np.uint8).reshape(k // 512, 16, n))


def unpack_weight(words, scales, fmt):
    g, _, n = scales.shape
    words = np.ascontiguousarray(words).reshape(g, 128, n, -1)
    if fmt == "e4m3":
        vals = words.view(ml_dtypes.float8_e4m3fn).astype(np.float64)
    else:
        nib = np.empty((g, 128, n, 4), np.uint8)
        nib[..., 0::2] = words & 0xF
        nib[..., 1::2] = words >> 4
        vals = E2M1[nib]
    vals = vals * np.repeat(np.exp2(scales.astype(np.float64) - 127.0), 8, axis=1)[..., None]
    return vals.transpose(0, 1, 3, 2).reshape(g * 512, n)


def gelu(v):
    return 0.5 * v * (1.0 + np.tanh(np.sqrt(2.0 / np.pi) * (v + 0.044715 * v**3)))


K, T, S, T2, S2, N = 512, 4096, 1536, 2048, 1024, 512

def setup_inputs():
    n = np.random.standard_normal
    s = mx_kscale(K)[:, None]
    u = mx_kscale(S)[:, None]
    tab_words, tab_scales = pack_weight(n((K, T)) / np.sqrt(K) * s, "e4m3")
    tab2_words, tab2_scales = pack_weight(n((K, T2)) / s, "e4m3")
    d_words, d_scales = pack_weight(np.exp(0.3 * n((S, N))) / S / u, "e2m1")
    w = unpack_weight(d_words, d_scales, "e2m1") * 8.0 * n((S, N))
    return {
        "tab_words": tab_words, "tab_scales": tab_scales,
        "tab2_words": tab2_words, "tab2_scales": tab2_scales,
        "offs": striped(np.random.permutation(T)[:S]),
        "offs2": striped(np.random.permutation(T2)[:S2]),
        "wg": (np.exp(0.3 * n(S)) * u[:, 0]).astype(np.float32),
        "w": w.astype(np.float32),
        "d_words": d_words, "d_scales": d_scales,
        "bn": (0.3 * n(N)).astype(np.float32),
    }

def reference(tab_words, tab_scales, tab2_words, tab2_scales, offs, offs2, wg, w, d_words, d_scales, bn):
    v = unpack_weight(tab_words, tab_scales, "e4m3")[:, unstriped(offs)]
    v2 = unpack_weight(tab2_words, tab2_scales, "e4m3")[:, unstriped(offs2)]
    a = v.T @ v2
    e = mxq(np.exp(a) * f64(wg)[:, None], 0, "e4m3")
    num = mxq(f64(w), 0, "e4m3").T @ e
    den = unpack_weight(d_words, d_scales, "e2m1").T @ e
    return num / den + f64(bn)[:, None]

@@ -1,0 +1,266 @@
+from contextlib import ExitStack
+
+import concourse.mybir as mybir
+
+K, T, S, T2, S2, N = 512, 4096, 1536, 2048, 1024, 512
+FLOPS = 2 * K * S * S2 + 2 * 2 * S * N * S2
+
+F32 = mybir.dt.float32
+BF16 = mybir.dt.bfloat16
+I32 = mybir.dt.int32
+U32 = mybir.dt.uint32
+U16 = mybir.dt.uint16
+U8 = mybir.dt.uint8
+FP8X4 = mybir.dt.float8_e4m3fn_x4
+FP4X4 = mybir.dt.float4_e2m1fn_x4
+ACT = mybir.ActivationFunctionType
+ALU = mybir.AluOpType
+
+P = 128
+PACK = 4
+PASS = P * PACK
+G = S // PASS
+CH = 512
+C = S2 // CH
+NT = N // P
+V_ROW = 8
+Q_ROW = 4
+
+
+def tile_list_replay_kernel_control_kernel(
+    tc, tab_words, tab_scales, tab2_words, tab2_scales, offs, offs2, wg, w, d_words, d_scales, bn, out
+):
+    nc = tc.nc
+    with ExitStack() as ctx:
+        keep = ctx.enter_context(tc.tile_pool(name="keep", bufs=1))
+        ring = ctx.enter_context(tc.tile_pool(name="ring", bufs=3))
+        psum = ctx.enter_context(tc.psum_pool(name="psum", bufs=1))
+
+        v_list = keep.tile([P, S // 16], U16, name="v_list")
+        q_list = keep.tile([P, S2 // 16], U16, name="q_list")
+        v_tab = keep.tile([P, T], I32, name="v_tab")
+        q_tab = keep.tile([P, T2], I32, name="q_tab")
+        v_tab_sc = keep.tile([P, T // 4], I32, name="v_tab_sc")
+        q_tab_sc = keep.tile([P, T2 // 4], I32, name="q_tab_sc")
+        d_sc = keep.tile([P, G, N // 4], I32, name="d_sc", align_bytes=64)
+        d_w = keep.tile([P, G, 2 * N // 4], I32, name="d_w", align_bytes=64)
+        wg_sb = keep.tile([P, G, PACK], F32, name="wg_sb")
+        ln_wg = keep.tile([P, G * PACK], F32, name="ln_wg", tag="late")
+        warm = keep.tile([P, 1], F32, name="warm")
+        bn_sb = keep.tile([P, NT], F32, name="bn_sb")
+        w_raw = [keep.tile([P, PACK, N], F32, name="w_raw%d" % g) for g in range(G)]
+
+        nc.vector.memset(q_tab_sc[:], 0)
+        nc.vector.memset(v_tab_sc[:], 0)
+        nc.vector.memset(d_sc[:], 0)
+
+        nc.sync.dma_start(q_list[:], offs2)
+        nc.sync.dma_start(v_list[:], offs)
+        nc.sync.dma_start(q_tab[:], tab2_words[0].rearrange("p t i -> p (t i)").bitcast(I32))
+        nc.sync.dma_start(v_tab[:], tab_words[0].rearrange("p t i -> p (t i)").bitcast(I32))
+        nc.gpsimd.dma_start(wg_sb[:], wg.rearrange("(g p t) -> p g t", p=P, t=PACK))
+        for q in range(4):
+            nc.scalar.dma_start(
+                q_tab_sc[32 * q + Q_ROW : 32 * q + Q_ROW + 4, :], tab2_scales[0, 4 * q : 4 * q + 4, :].bitcast(I32)
+            )
+        for q in range(4):
+            nc.scalar.dma_start(
+                v_tab_sc[32 * q + V_ROW : 32 * q + V_ROW + 4, :], tab_scales[0, 4 * q : 4 * q + 4, :].bitcast(I32)
+            )
+        for g in range(G):
+            nc.sync.dma_start(w_raw[g][:], w[g * PASS : (g + 1) * PASS, :].rearrange("(p t) n -> p t n", t=PACK))
+        nc.sync.dma_start(d_w[:], d_words.rearrange("g p b -> p g b").bitcast(I32))
+        for q in range(4):
+            nc.sync.dma_start(
+                d_sc[32 * q : 32 * q + 4, :, :],
+                d_scales[:, 4 * q : 4 * q + 4, :].rearrange("g r n -> r g n").bitcast(I32),
+            )
+        with nc.allow_non_contiguous_dma(reason="one bias value a partition"):
+            nc.sync.dma_start(bn_sb[:], bn.rearrange("(c p) -> p c", p=P))
+
+        nc.scalar.activation(ln_wg[:], wg_sb[:].rearrange("p g t -> p (g t)"), ACT.Ln)
+        nc.scalar.activation(warm[:], ln_wg[:, 0:1], ACT.Exp)
+
+        q_w = [keep.tile([P, CH], U32, name="q_w%d" % c, align_bytes=64) for c in range(C)]
+        q_s = [keep.tile([P, CH], U8, name="q_s%d" % c, align_bytes=64) for c in range(C)]
+        v_w = [keep.tile([P, PASS], U32, name="v_w%d" % g, align_bytes=64) for g in range(G)]
+        v_s_list = [keep.tile([P, PASS], U8, name="v_s_list%d" % g, align_bytes=64) for g in range(G)]
+        v_s = [keep.tile([P, PASS], U8, name="v_s%d" % g, align_bytes=64) for g in range(G)]
+        e_w = {(g, c): keep.tile([P, CH], U32, name="e_w%d%d" % (g, c), align_bytes=64) for g in range(G) for c in range(C)}
+        e_s = {(g, c): keep.tile([P, CH], U8, name="e_s%d%d" % (g, c), align_bytes=64) for g in range(G) for c in range(C)}
+        planes = {(g, c): keep.tile([P, PACK, CH], BF16, name="planes%d%d" % (g, c)) for g in range(G) for c in range(C)}
+        w_w = [keep.tile([P, N], U32, name="w_w%d" % g, align_bytes=64) for g in range(G)]
+        w_s = [keep.tile([P, N], U8, name="w_s%d" % g, align_bytes=64) for g in range(G)]
+        w_bf = [keep.tile([P, N, PACK], BF16, name="w_bf%d" % g, align_bytes=64) for g in range(G)]
+        den_sq = {(n, c): keep.tile([P, CH], F32, name="den_sq%d%d" % (n, c)) for n in range(NT) for c in range(C)}
+
+        def bank(b):
+            return psum.tile([P, CH], F32, name="bank%d" % b, tag="bank%d" % b)
+
+        def cols(k):
+            return slice(k * CH // 16, (k + 1) * CH // 16)
+
+        def gather_q_scales(c):
+            nc.vector.tensor_copy(q_s[c][:], q_tab_sc[:].bitcast(U8).indirect(q_list[:, cols(c)]))
+
+        def gather_q_words(c):
+            nc.vector.tensor_copy(q_w[c][:], q_tab[:].bitcast(U32).indirect(q_list[:, cols(c)]))
+
+        def gather_v_scales(g):
+            nc.vector.tensor_copy(v_s_list[g][:], v_tab_sc[:].bitcast(U8).indirect(v_list[:, cols(g)]))
+
+        def order_v_scales(g):
+            nc.vector.tensor_copy(
+                v_s[g][:].rearrange("p (t m) -> p m t", t=PACK), v_s_list[g][:].rearrange("p (m t) -> p m t", t=PACK)
+            )
+
+        def gather_v_words(g):
+            nc.vector.tensor_copy(
+                v_w[g][:].rearrange("p (t m) -> p m t", t=PACK), v_tab[:].bitcast(U32).indirect(v_list[:, cols(g)])
+            )
+
+        a_count = [0]
+
+        def kernel_values(g, c):
+            for t in range(PACK):
+                acc = bank(a_count[0] % 3)
+                a_count[0] += 1
+                m = slice(t * P, (t + 1) * P)
+                nc.tensor.matmul_mx(
+                    out=acc[:],
+                    lhsT=v_w[g][:, m].bitcast(FP8X4),
+                    lhsT_scale=v_s[g][V_ROW:P, m],
+                    rhs=q_w[c][:].bitcast(FP8X4),
+                    rhs_scale=q_s[c][Q_ROW:P, :],
+                    start=True,
+                    stop=True,
+                )
+                col = g * PACK + t
+                nc.scalar.activation(planes[g, c][:, t, :], acc[:], ACT.Exp, bias=ln_wg[:, col : col + 1])
+
+        e_bf = {}
+
+        def interleave_e(g, c):
+            e_bf[g, c] = ring.tile([P, CH, PACK], BF16, name="e_bf", align_bytes=64)
+            nc.vector.tensor_copy(
+                e_bf[g, c][:].rearrange("p (c i) t -> p c t i", i=4),
+                planes[g, c][:].rearrange("p t (c i) -> p c t i", i=4),
+            )
+
+        def quantize_e(g, c):
+            nc.vector.quantize_mx(
+                out=e_w[g, c][:].bitcast(FP8X4), scales=e_s[g, c][:], in_=e_bf[g, c][:].rearrange("p j t -> p (j t)")
+            )
+
+        def cast_w(g, on_scalar):
+            src = w_raw[g][:].rearrange("p t n -> p n t")
+            if on_scalar:
+                nc.scalar.copy(w_bf[g][:], src)
+            else:
+                nc.vector.tensor_copy(w_bf[g][:], src)
+
+        def quantize_w(g):
+            nc.vector.quantize_mx(
+                out=w_w[g][:].bitcast(FP8X4), scales=w_s[g][:], in_=w_bf[g][:].rearrange("p n t -> p (n t)")
+            )
+
+        def den_pass(acc, n, c, g):
+            nc.tensor.matmul_mx(
+                out=acc[:],
+                lhsT=d_w[:, g, n * 64 : (n + 1) * 64].bitcast(U8).bitcast(FP4X4),
+                lhsT_scale=d_sc[:, g, n * 32 : (n + 1) * 32].bitcast(U8),
+                rhs=e_w[g, c][:].bitcast(FP8X4),
+                rhs_scale=e_s[g, c][:],
+                start=(g == 0),
+                stop=(g == G - 1),
+            )
+
+        def num_pass(acc, n, c, g):
+            m = slice(n * P, (n + 1) * P)
+            nc.tensor.matmul_mx(
+                out=acc[:],
+                lhsT=w_w[g][:, m].bitcast(FP8X4),
+                lhsT_scale=w_s[g][:, m],
+                rhs=e_w[g, c][:].bitcast(FP8X4),
+                rhs_scale=e_s[g, c][:],
+                start=(g == 0),
+                stop=(g == G - 1),
+            )
+
+        def den_tile(n, c, b):
+            acc = bank(b)
+            for g in range(G):
+                den_pass(acc, n, c, g)
+            nc.scalar.activation(den_sq[n, c][:], acc[:], ACT.Square)
+
+        num = {}
+
+        def num_tile(n, c, b):
+            num[n, c] = bank(b)
+            for g in range(G):
+                num_pass(num[n, c], n, c, g)
+
+        gather_q_scales(0)
+        gather_v_scales(0)
+        gather_q_words(0)
+        order_v_scales(0)
+        gather_v_scales(1)
+        gather_v_words(0)
+        order_v_scales(1)
+        kernel_values(0, 0)
+        gather_v_words(1)
+        gather_v_scales(2)
+        kernel_values(1, 0)
+        gather_v_words(2)
+        order_v_scales(2)
+        cast_w(0, True)
+        kernel_values(2, 0)
+        gather_q_scales(1)
+        gather_q_words(1)
+        interleave_e(0, 0)
+        interleave_e(1, 0)
+        quantize_e(0, 0)
+        kernel_values(0, 1)
+        interleave_e(2, 0)
+        quantize_e(1, 0)
+        quantize_w(0)
+        quantize_e(2, 0)
+        kernel_values(1, 1)
+        cast_w(1, False)
+        cast_w(2, False)
+        quantize_w(1)
+        den_tile(0, 0, 3)
+        interleave_e(0, 1)
+        quantize_w(2)
+        kernel_values(2, 1)
+        interleave_e(1, 1)
+        quantize_e(0, 1)
+        interleave_e(2, 1)
+        quantize_e(1, 1)
+        quantize_e(2, 1)
+        num_tile(0, 0, 4)
+        den_tile(1, 0, 3)
+        num_tile(1, 0, 5)
+        den_tile(2, 0, 0)
+        num_tile(2, 0, 6)
+        den_tile(3, 0, 1)
+        num_tile(3, 0, 7)
+
+        rec = keep.tile([P, NT * C, CH], F32, name="rec", tag="late")
+
+        def finish(n, c, last):
+            r = rec[:, c * NT + n, :]
+            nc.scalar.activation(r, den_sq[n, c][:], ACT.Abs_reciprocal_sqrt)
+            ratio = ring.tile([P, CH], F32, name="ratio")
+            nc.vector.tensor_tensor(ratio[:], num[n, c][:], r, ALU.mult)
+            res = ring.tile([P, CH], F32, name="res")
+            eng = nc.vector if last else nc.gpsimd
+            eng.tensor_scalar(res[:], ratio[:], 1.0, bn_sb[:, n : n + 1], ALU.mult, ALU.add)
+            nc.sync.dma_start(out[n * P : (n + 1) * P, c * CH : (c + 1) * CH], res[:])
+
+        for n in range(NT):
+            finish(n, 0, False)
+            den_tile(n, 1, (2, 3, 0, 1)[n])
+            num_tile(n, 1, 4 + n)
+        for n in range(NT):
+            finish(n, 1, n == NT - 1)

@@ -17,14 +17,25 @@ ACT = mybir.ActivationFunctionType
 ALU = mybir.AluOpType
 
 P = 128
-PACK = 4
-PASS = P * PACK
-G = S // PASS
-CH = 512
-C = S2 // CH
-NT = N // P
+SLOTS = 4
+PASS = P * SLOTS
+PASSES = S // PASS
+CHUNK = 512
+CHUNKS = S2 // CHUNK
+N_TILES = N // P
+LIST_COLS = PASS // 16
+RUN = 4
+ALIGN = 64
+
 V_ROW = 8
 Q_ROW = 4
+
+A_BANKS = 3
+DEN_BANKS = (3, 4, 5, 6)
+NUM_BANKS = (7, 0, 1, 2)
+
+TWICE = 0
+HALVED = 2
 
 
 def tile_list_replay_kernel_control_kernel(
@@ -36,231 +47,252 @@ def tile_list_replay_kernel_control_kernel(
         ring = ctx.enter_context(tc.tile_pool(name="ring", bufs=3))
         psum = ctx.enter_context(tc.psum_pool(name="psum", bufs=1))
 
+        def bank(b):
+            return psum.tile([P, CHUNK], F32, name="bank%d" % b, tag="bank%d" % b)
+
+        def load_scale_rows(dst, first_row, rows):
+            for r in range(4):
+                nc.sync.dma_start(dst[first_row + r : P : 32], rows[r:16:4].bitcast(I32))
+
         v_list = keep.tile([P, S // 16], U16, name="v_list")
         q_list = keep.tile([P, S2 // 16], U16, name="q_list")
-        v_tab = keep.tile([P, T], I32, name="v_tab")
-        q_tab = keep.tile([P, T2], I32, name="q_tab")
-        v_tab_sc = keep.tile([P, T // 4], I32, name="v_tab_sc")
-        q_tab_sc = keep.tile([P, T2 // 4], I32, name="q_tab_sc")
-        d_sc = keep.tile([P, G, N // 4], I32, name="d_sc", align_bytes=64)
-        d_w = keep.tile([P, G, 2 * N // 4], I32, name="d_w", align_bytes=64)
-        wg_sb = keep.tile([P, G, PACK], F32, name="wg_sb")
-        ln_wg = keep.tile([P, G * PACK], F32, name="ln_wg", tag="late")
-        warm = keep.tile([P, 1], F32, name="warm")
-        bn_sb = keep.tile([P, NT], F32, name="bn_sb")
-        w_raw = [keep.tile([P, PACK, N], F32, name="w_raw%d" % g) for g in range(G)]
+        v_tab_scales = keep.tile([P, T // 4], I32, name="v_tab_scales", tag="q_words1", align_bytes=ALIGN)
+        q_tab_scales = keep.tile([P, T2 // 4], I32, name="q_tab_scales")
+        d_scale_rows = keep.tile([P, PASSES, N // 4], I32, name="d_scale_rows", align_bytes=ALIGN)
+        wg_sb = keep.tile([P, PASSES, SLOTS], F32, name="wg_sb")
+        ln_wg = keep.tile([P, PASSES * SLOTS], F32, name="ln_wg", tag="recip")
+        ln_wg_first = keep.tile([P, 1], F32, name="ln_wg_first", tag="d_codes", align_bytes=ALIGN)
+        warm = keep.tile([P, 1], F32, name="warm", tag="w_raw0", align_bytes=ALIGN)
+        one = keep.tile([P, 1], F32, name="one", tag="v_tab_words")
 
-        nc.vector.memset(q_tab_sc[:], 0)
-        nc.vector.memset(v_tab_sc[:], 0)
-        nc.vector.memset(d_sc[:], 0)
+        nc.gpsimd.memset(q_tab_scales[:], 0)
+        nc.gpsimd.memset(one[:], 1.0)
+        nc.vector.memset(v_tab_scales[:], 0)
+        nc.vector.memset(d_scale_rows[:], 0)
 
         nc.sync.dma_start(q_list[:], offs2)
         nc.sync.dma_start(v_list[:], offs)
-        nc.sync.dma_start(q_tab[:], tab2_words[0].rearrange("p t i -> p (t i)").bitcast(I32))
-        nc.sync.dma_start(v_tab[:], tab_words[0].rearrange("p t i -> p (t i)").bitcast(I32))
-        nc.gpsimd.dma_start(wg_sb[:], wg.rearrange("(g p t) -> p g t", p=P, t=PACK))
-        for q in range(4):
-            nc.scalar.dma_start(
-                q_tab_sc[32 * q + Q_ROW : 32 * q + Q_ROW + 4, :], tab2_scales[0, 4 * q : 4 * q + 4, :].bitcast(I32)
-            )
-        for q in range(4):
-            nc.scalar.dma_start(
-                v_tab_sc[32 * q + V_ROW : 32 * q + V_ROW + 4, :], tab_scales[0, 4 * q : 4 * q + 4, :].bitcast(I32)
-            )
-        for g in range(G):
-            nc.sync.dma_start(w_raw[g][:], w[g * PASS : (g + 1) * PASS, :].rearrange("(p t) n -> p t n", t=PACK))
-        nc.sync.dma_start(d_w[:], d_words.rearrange("g p b -> p g b").bitcast(I32))
-        for q in range(4):
-            nc.sync.dma_start(
-                d_sc[32 * q : 32 * q + 4, :, :],
-                d_scales[:, 4 * q : 4 * q + 4, :].rearrange("g r n -> r g n").bitcast(I32),
-            )
-        with nc.allow_non_contiguous_dma(reason="one bias value a partition"):
-            nc.sync.dma_start(bn_sb[:], bn.rearrange("(c p) -> p c", p=P))
+        nc.sync.dma_start(wg_sb[:], wg.rearrange("(g p t) -> p g t", p=P, t=SLOTS))
+        load_scale_rows(q_tab_scales, Q_ROW, tab2_scales[0])
+        q_tab_words = keep.tile([P, T2], I32, name="q_tab_words", tag="q_tab_words")
+        nc.sync.dma_start(q_tab_words[:], tab2_words[0].rearrange("p t i -> p (t i)").bitcast(I32))
+        load_scale_rows(v_tab_scales, V_ROW, tab_scales[0])
 
+        nc.scalar.activation(warm[:], one[:], ACT.Ln)
+        v_tab_words = keep.tile([P, T], I32, name="v_tab_words", tag="v_tab_words")
+        nc.sync.dma_start(v_tab_words[:], tab_words[0].rearrange("p t i -> p (t i)").bitcast(I32))
+        load_scale_rows(d_scale_rows, 0, d_scales.rearrange("g r n -> r g n"))
+
+        nc.scalar.activation(ln_wg_first[:], wg_sb[:, 0, 0:1], ACT.Ln)
         nc.scalar.activation(ln_wg[:], wg_sb[:].rearrange("p g t -> p (g t)"), ACT.Ln)
         nc.scalar.activation(warm[:], ln_wg[:, 0:1], ACT.Exp)
 
-        q_w = [keep.tile([P, CH], U32, name="q_w%d" % c, align_bytes=64) for c in range(C)]
-        q_s = [keep.tile([P, CH], U8, name="q_s%d" % c, align_bytes=64) for c in range(C)]
-        v_w = [keep.tile([P, PASS], U32, name="v_w%d" % g, align_bytes=64) for g in range(G)]
-        v_s_list = [keep.tile([P, PASS], U8, name="v_s_list%d" % g, align_bytes=64) for g in range(G)]
-        v_s = [keep.tile([P, PASS], U8, name="v_s%d" % g, align_bytes=64) for g in range(G)]
-        e_w = {(g, c): keep.tile([P, CH], U32, name="e_w%d%d" % (g, c), align_bytes=64) for g in range(G) for c in range(C)}
-        e_s = {(g, c): keep.tile([P, CH], U8, name="e_s%d%d" % (g, c), align_bytes=64) for g in range(G) for c in range(C)}
-        planes = {(g, c): keep.tile([P, PACK, CH], BF16, name="planes%d%d" % (g, c)) for g in range(G) for c in range(C)}
-        w_w = [keep.tile([P, N], U32, name="w_w%d" % g, align_bytes=64) for g in range(G)]
-        w_s = [keep.tile([P, N], U8, name="w_s%d" % g, align_bytes=64) for g in range(G)]
-        w_bf = [keep.tile([P, N, PACK], BF16, name="w_bf%d" % g, align_bytes=64) for g in range(G)]
-        den_sq = {(n, c): keep.tile([P, CH], F32, name="den_sq%d%d" % (n, c)) for n in range(NT) for c in range(C)}
+        q_words, q_scales, v_words, v_scales_listed, w_raw, e_bf, den, num = {}, {}, {}, {}, {}, {}, {}, {}
+        units = [(g, c) for g in range(PASSES) for c in range(CHUNKS)]
+        v_scales = [keep.tile([P, PASS], U8, name="v_scales%d" % g, align_bytes=ALIGN) for g in range(PASSES)]
+        e_words = {u: keep.tile([P, CHUNK], U32, name="e_words%d%d" % u, align_bytes=ALIGN) for u in units}
+        e_scales = {u: keep.tile([P, CHUNK], U8, name="e_scales%d%d" % u, align_bytes=ALIGN) for u in units}
+        e_rows = {u: keep.tile([P, SLOTS, CHUNK], BF16, name="e_rows%d%d" % u) for u in units}
+        w_words = [keep.tile([P, N], U32, name="w_words%d" % g, align_bytes=ALIGN) for g in range(PASSES)]
+        w_scales = [keep.tile([P, N], U8, name="w_scales%d" % g, align_bytes=ALIGN) for g in range(PASSES)]
+        w_bf = [keep.tile([P, N, SLOTS], BF16, name="w_bf%d" % g, align_bytes=ALIGN) for g in range(PASSES)]
+        scratch = {
+            (n, c): keep.tile([P, CHUNK], F32, name="scratch%d%d" % (n, c))
+            for n in range(N_TILES)
+            for c in range(CHUNKS)
+        }
 
-        def bank(b):
-            return psum.tile([P, CH], F32, name="bank%d" % b, tag="bank%d" % b)
-
-        def cols(k):
-            return slice(k * CH // 16, (k + 1) * CH // 16)
+        def entries(k):
+            return slice(k * LIST_COLS, (k + 1) * LIST_COLS)
 
         def gather_q_scales(c):
-            nc.vector.tensor_copy(q_s[c][:], q_tab_sc[:].bitcast(U8).indirect(q_list[:, cols(c)]))
+            q_scales[c] = keep.tile([P, CHUNK], U8, name="q_scales%d" % c, align_bytes=ALIGN)
+            nc.vector.tensor_copy(q_scales[c][:], q_tab_scales[:].bitcast(U8).indirect(q_list[:, entries(c)]))
 
         def gather_q_words(c):
-            nc.vector.tensor_copy(q_w[c][:], q_tab[:].bitcast(U32).indirect(q_list[:, cols(c)]))
+            q_words[c] = keep.tile([P, CHUNK], U32, name="q_words%d" % c, tag="q_words%d" % c, align_bytes=ALIGN)
+            nc.vector.tensor_copy(q_words[c][:], q_tab_words[:].bitcast(U32).indirect(q_list[:, entries(c)]))
 
         def gather_v_scales(g):
-            nc.vector.tensor_copy(v_s_list[g][:], v_tab_sc[:].bitcast(U8).indirect(v_list[:, cols(g)]))
+            tag = ("w_raw1", "w_raw2", "d_codes")[g]
+            v_scales_listed[g] = keep.tile([P, PASS], U8, name="v_scales_listed%d" % g, tag=tag, align_bytes=ALIGN)
+            nc.vector.tensor_copy(v_scales_listed[g][:], v_tab_scales[:].bitcast(U8).indirect(v_list[:, entries(g)]))
 
         def order_v_scales(g):
             nc.vector.tensor_copy(
-                v_s[g][:].rearrange("p (t m) -> p m t", t=PACK), v_s_list[g][:].rearrange("p (m t) -> p m t", t=PACK)
+                v_scales[g][:].rearrange("p (t m) -> p t m", t=SLOTS),
+                v_scales_listed[g][:].rearrange("p (m t) -> p t m", t=SLOTS),
             )
 
         def gather_v_words(g):
+            v_words[g] = keep.tile([P, PASS], U32, name="v_words%d" % g, align_bytes=ALIGN)
             nc.vector.tensor_copy(
-                v_w[g][:].rearrange("p (t m) -> p m t", t=PACK), v_tab[:].bitcast(U32).indirect(v_list[:, cols(g)])
+                v_words[g][:].rearrange("p (t m) -> p m t", t=SLOTS),
+                v_tab_words[:].bitcast(U32).indirect(v_list[:, entries(g)]),
             )
 
-        a_count = [0]
+        def load_w(g):
+            w_raw[g] = keep.tile([P, SLOTS, N], F32, name="w_raw%d" % g, tag="w_raw%d" % g, align_bytes=ALIGN)
+            nc.sync.dma_start(w_raw[g][:], w[g * PASS : (g + 1) * PASS, :].rearrange("(p t) n -> p t n", t=SLOTS))
 
-        def kernel_values(g, c):
-            for t in range(PACK):
-                acc = bank(a_count[0] % 3)
-                a_count[0] += 1
-                m = slice(t * P, (t + 1) * P)
-                nc.tensor.matmul_mx(
-                    out=acc[:],
-                    lhsT=v_w[g][:, m].bitcast(FP8X4),
-                    lhsT_scale=v_s[g][V_ROW:P, m],
-                    rhs=q_w[c][:].bitcast(FP8X4),
-                    rhs_scale=q_s[c][Q_ROW:P, :],
-                    start=True,
-                    stop=True,
+        def interleave(dst, src):
+            nc.vector.tensor_copy(
+                dst.rearrange("p (c i) t -> p c t i", i=RUN), src.rearrange("p t (c i) -> p c t i", i=RUN)
+            )
+
+        def round_w_on_gpsimd(g):
+            for h in range(2):
+                ns = slice(h * N // 2, (h + 1) * N // 2)
+                nc.gpsimd.tensor_scalar(
+                    w_bf[g][:, ns, :], w_raw[g][:, :, ns].rearrange("p t n -> p n t"), 1.0, 0.0, ALU.mult, ALU.add
                 )
-                col = g * PACK + t
-                nc.scalar.activation(planes[g, c][:, t, :], acc[:], ACT.Exp, bias=ln_wg[:, col : col + 1])
 
-        e_bf = {}
-
-        def interleave_e(g, c):
-            e_bf[g, c] = ring.tile([P, CH, PACK], BF16, name="e_bf", align_bytes=64)
-            nc.vector.tensor_copy(
-                e_bf[g, c][:].rearrange("p (c i) t -> p c t i", i=4),
-                planes[g, c][:].rearrange("p t (c i) -> p c t i", i=4),
-            )
-
-        def quantize_e(g, c):
-            nc.vector.quantize_mx(
-                out=e_w[g, c][:].bitcast(FP8X4), scales=e_s[g, c][:], in_=e_bf[g, c][:].rearrange("p j t -> p (j t)")
-            )
-
-        def cast_w(g, on_scalar):
-            src = w_raw[g][:].rearrange("p t n -> p n t")
-            if on_scalar:
-                nc.scalar.copy(w_bf[g][:], src)
-            else:
-                nc.vector.tensor_copy(w_bf[g][:], src)
+        def round_w(g):
+            interleave(w_bf[g][:], w_raw[g][:])
 
         def quantize_w(g):
             nc.vector.quantize_mx(
-                out=w_w[g][:].bitcast(FP8X4), scales=w_s[g][:], in_=w_bf[g][:].rearrange("p n t -> p (n t)")
+                out=w_words[g][:].bitcast(FP8X4), scales=w_scales[g][:], in_=w_bf[g][:].rearrange("p n t -> p (n t)")
             )
 
-        def den_pass(acc, n, c, g):
-            nc.tensor.matmul_mx(
-                out=acc[:],
-                lhsT=d_w[:, g, n * 64 : (n + 1) * 64].bitcast(U8).bitcast(FP4X4),
-                lhsT_scale=d_sc[:, g, n * 32 : (n + 1) * 32].bitcast(U8),
-                rhs=e_w[g, c][:].bitcast(FP8X4),
-                rhs_scale=e_s[g, c][:],
-                start=(g == 0),
-                stop=(g == G - 1),
+        def kernel_values(g, c):
+            for t in range(SLOTS):
+                acc = bank(((c * PASSES + g) * SLOTS + t) % A_BANKS)
+                m = slice(t * P, (t + 1) * P)
+                nc.tensor.matmul_mx(
+                    out=acc[:],
+                    lhsT=v_words[g][:, m].bitcast(FP8X4),
+                    lhsT_scale=v_scales[g][V_ROW:P, m],
+                    rhs=q_words[c][:].bitcast(FP8X4),
+                    rhs_scale=q_scales[c][Q_ROW:P, :],
+                    start=True,
+                    stop=True,
+                )
+                col = g * SLOTS + t
+                bias = ln_wg_first[:] if (g, c, t) == (0, 0, 0) else ln_wg[:, col : col + 1]
+                nc.scalar.activation(e_rows[g, c][:, t, :], acc[:], ACT.Exp, bias=bias)
+
+        def interleave_e(g, c):
+            e_bf[g, c] = ring.tile([P, CHUNK, SLOTS], BF16, name="e_bf", align_bytes=ALIGN)
+            interleave(e_bf[g, c][:], e_rows[g, c][:])
+
+        def quantize_e(g, c):
+            nc.vector.quantize_mx(
+                out=e_words[g, c][:].bitcast(FP8X4),
+                scales=e_scales[g, c][:],
+                in_=e_bf[g, c][:].rearrange("p j t -> p (j t)"),
             )
 
-        def num_pass(acc, n, c, g):
-            m = slice(n * P, (n + 1) * P)
-            nc.tensor.matmul_mx(
-                out=acc[:],
-                lhsT=w_w[g][:, m].bitcast(FP8X4),
-                lhsT_scale=w_s[g][:, m],
-                rhs=e_w[g, c][:].bitcast(FP8X4),
-                rhs_scale=e_s[g, c][:],
-                start=(g == 0),
-                stop=(g == G - 1),
-            )
-
-        def den_tile(n, c, b):
-            acc = bank(b)
-            for g in range(G):
-                den_pass(acc, n, c, g)
-            nc.scalar.activation(den_sq[n, c][:], acc[:], ACT.Square)
-
-        num = {}
-
-        def num_tile(n, c, b):
-            num[n, c] = bank(b)
-            for g in range(G):
-                num_pass(num[n, c], n, c, g)
-
+        load_w(0)
         gather_q_scales(0)
-        gather_v_scales(0)
         gather_q_words(0)
+        gather_v_scales(0)
         order_v_scales(0)
-        gather_v_scales(1)
+        load_w(1)
         gather_v_words(0)
-        order_v_scales(1)
+        gather_v_scales(1)
         kernel_values(0, 0)
+        order_v_scales(1)
+        load_w(2)
         gather_v_words(1)
         gather_v_scales(2)
         kernel_values(1, 0)
         gather_v_words(2)
         order_v_scales(2)
-        cast_w(0, True)
+        d_codes = keep.tile([P, PASSES, 2 * N // 4], I32, name="d_codes", tag="d_codes", align_bytes=ALIGN)
+        nc.sync.dma_start(d_codes[:], d_words.rearrange("g p b -> p g b").bitcast(I32))
         kernel_values(2, 0)
         gather_q_scales(1)
         gather_q_words(1)
+        bn_sb = keep.tile([P, N_TILES], F32, name="bn_sb", tag="q_tab_words")
+        with nc.allow_non_contiguous_dma(reason="one bias value a partition and row tile"):
+            nc.sync.dma_start(bn_sb[:], bn.rearrange("(n p) -> p n", p=P))
+        for g in range(PASSES):
+            kernel_values(g, 1)
+
+        def den_passes(c, passes):
+            for n in range(N_TILES):
+                if passes[0] == 0:
+                    den[n, c] = bank(DEN_BANKS[n])
+                for g in passes:
+                    nc.tensor.matmul_mx(
+                        out=den[n, c][:],
+                        lhsT=d_codes[:, g, n * 2 * P // 4 : (n + 1) * 2 * P // 4].bitcast(U8).bitcast(FP4X4),
+                        lhsT_scale=d_scale_rows[:, g, n * P // 4 : (n + 1) * P // 4].bitcast(U8),
+                        rhs=e_words[g, c][:].bitcast(FP8X4),
+                        rhs_scale=e_scales[g, c][:],
+                        start=(g == 0),
+                        stop=(g == PASSES - 1),
+                    )
+
+        def num_tile(n, c):
+            num[n, c] = bank(NUM_BANKS[n])
+            m = slice(n * P, (n + 1) * P)
+            for g in range(PASSES):
+                nc.tensor.matmul_mx(
+                    out=num[n, c][:],
+                    lhsT=w_words[g][:, m].bitcast(FP8X4),
+                    lhsT_scale=w_scales[g][:, m],
+                    rhs=e_words[g, c][:].bitcast(FP8X4),
+                    rhs_scale=e_scales[g, c][:],
+                    start=(g == 0),
+                    stop=(g == PASSES - 1),
+                )
+
+        def square_den(n, c):
+            nc.scalar.activation(scratch[n, c][:], den[n, c][:], ACT.Square)
+
+        round_w_on_gpsimd(0)
         interleave_e(0, 0)
         interleave_e(1, 0)
         quantize_e(0, 0)
-        kernel_values(0, 1)
         interleave_e(2, 0)
         quantize_e(1, 0)
-        quantize_w(0)
+        round_w(1)
         quantize_e(2, 0)
-        kernel_values(1, 1)
-        cast_w(1, False)
-        cast_w(2, False)
+        den_passes(0, [0, 1, 2])
+        for n in range(N_TILES):
+            square_den(n, 0)
+        quantize_w(0)
+        round_w(2)
         quantize_w(1)
-        den_tile(0, 0, 3)
         interleave_e(0, 1)
         quantize_w(2)
-        kernel_values(2, 1)
+        for n in range(N_TILES):
+            num_tile(n, 0)
         interleave_e(1, 1)
         quantize_e(0, 1)
-        interleave_e(2, 1)
+        den_passes(1, [0])
         quantize_e(1, 1)
+        den_passes(1, [1])
+        interleave_e(2, 1)
         quantize_e(2, 1)
-        num_tile(0, 0, 4)
-        den_tile(1, 0, 3)
-        num_tile(1, 0, 5)
-        den_tile(2, 0, 0)
-        num_tile(2, 0, 6)
-        den_tile(3, 0, 1)
-        num_tile(3, 0, 7)
+        den_passes(1, [2])
 
-        rec = keep.tile([P, NT * C, CH], F32, name="rec", tag="late")
+        recip = keep.tile([P, N_TILES * CHUNKS, CHUNK], F32, name="recip", tag="recip")
 
-        def finish(n, c, last):
-            r = rec[:, c * NT + n, :]
-            nc.scalar.activation(r, den_sq[n, c][:], ACT.Abs_reciprocal_sqrt)
-            ratio = ring.tile([P, CH], F32, name="ratio")
-            nc.vector.tensor_tensor(ratio[:], num[n, c][:], r, ALU.mult)
-            res = ring.tile([P, CH], F32, name="res")
-            eng = nc.vector if last else nc.gpsimd
-            eng.tensor_scalar(res[:], ratio[:], 1.0, bn_sb[:, n : n + 1], ALU.mult, ALU.add)
-            nc.sync.dma_start(out[n * P : (n + 1) * P, c * CH : (c + 1) * CH], res[:])
+        def finish(n, c, twice, halved):
+            r = recip[:, c * N_TILES + n, :]
+            radicand = den[n, c] if twice else scratch[n, c]
+            ratio = keep.tile([P, CHUNK], F32, name="ratio%d%d" % (n, c))
+            res = keep.tile([P, CHUNK], F32, name="res%d%d" % (n, c))
+            width = CHUNK // 2 if halved else CHUNK
+            parts = [slice(j0, j0 + width) for j0 in range(0, CHUNK, width)]
+            for j in parts:
+                nc.scalar.activation(r[:, j], radicand[:, j], ACT.Abs_reciprocal_sqrt)
+                nc.vector.tensor_tensor(ratio[:, j], num[n, c][:, j], r[:, j], ALU.mult)
+            if twice:
+                nc.vector.tensor_tensor(scratch[n, c][:], ratio[:], r, ALU.mult)
+                ratio = scratch[n, c]
+            adder = nc.vector if halved else nc.gpsimd
+            for j in parts:
+                adder.tensor_scalar(res[:, j], ratio[:, j], 1.0, bn_sb[:, n : n + 1], ALU.mult, ALU.add)
+                nc.sync.dma_start(out[n * P : (n + 1) * P, c * CHUNK + j.start : c * CHUNK + j.stop], res[:, j])
 
-        for n in range(NT):
-            finish(n, 0, False)
-            den_tile(n, 1, (2, 3, 0, 1)[n])
-            num_tile(n, 1, 4 + n)
-        for n in range(NT):
-            finish(n, 1, n == NT - 1)
+        for n in range(N_TILES):
+            finish(n, 0, False, False)
+            num_tile(n, 1)
+        for n in range(N_TILES):
+            if n != TWICE:
+                square_den(n, 1)
+            finish(n, 1, n == TWICE, n >= HALVED)

@@ -30,12 +30,13 @@ ALIGN = 64
 V_ROW = 8
 Q_ROW = 4
 
-A_BANKS = 3
-DEN_BANKS = (3, 4, 5, 6)
-NUM_BANKS = (7, 0, 1, 2)
+BANKS = 8
+NARROW_FROM = 8
+NUM_BANKS = ((0, 1, 2, 3), (5, 7, 2, 3))
+DEN_BANKS = ((4, 5, 6, 7), (4, 6, 0, 1))
 
-TWICE = 0
-HALVED = 2
+TWICE = 2
+HALVED = 3
 
 
 def tile_list_replay_kernel_control_kernel(
@@ -57,18 +58,14 @@ def tile_list_replay_kernel_control_kernel(
         v_list = keep.tile([P, S // 16], U16, name="v_list")
         q_list = keep.tile([P, S2 // 16], U16, name="q_list")
         v_tab_scales = keep.tile([P, T // 4], I32, name="v_tab_scales", tag="q_words1", align_bytes=ALIGN)
-        q_tab_scales = keep.tile([P, T2 // 4], I32, name="q_tab_scales")
-        d_scale_rows = keep.tile([P, PASSES, N // 4], I32, name="d_scale_rows", align_bytes=ALIGN)
-        wg_sb = keep.tile([P, PASSES, SLOTS], F32, name="wg_sb")
+        q_tab_scales = keep.tile([P, T2 // 4], I32, name="q_tab_scales", tag="d_scale_rows", align_bytes=ALIGN)
+        wg_sb = keep.tile([P, PASSES, SLOTS], F32, name="wg_sb", tag="v_tab_words")
         ln_wg = keep.tile([P, PASSES * SLOTS], F32, name="ln_wg", tag="recip")
         ln_wg_first = keep.tile([P, 1], F32, name="ln_wg_first", tag="d_codes", align_bytes=ALIGN)
         warm = keep.tile([P, 1], F32, name="warm", tag="w_raw0", align_bytes=ALIGN)
-        one = keep.tile([P, 1], F32, name="one", tag="v_tab_words")
 
         nc.gpsimd.memset(q_tab_scales[:], 0)
-        nc.gpsimd.memset(one[:], 1.0)
         nc.vector.memset(v_tab_scales[:], 0)
-        nc.vector.memset(d_scale_rows[:], 0)
 
         nc.sync.dma_start(q_list[:], offs2)
         nc.sync.dma_start(v_list[:], offs)
@@ -78,24 +75,25 @@ def tile_list_replay_kernel_control_kernel(
         nc.sync.dma_start(q_tab_words[:], tab2_words[0].rearrange("p t i -> p (t i)").bitcast(I32))
         load_scale_rows(v_tab_scales, V_ROW, tab_scales[0])
 
-        nc.scalar.activation(warm[:], one[:], ACT.Ln)
-        v_tab_words = keep.tile([P, T], I32, name="v_tab_words", tag="v_tab_words")
-        nc.sync.dma_start(v_tab_words[:], tab_words[0].rearrange("p t i -> p (t i)").bitcast(I32))
-        load_scale_rows(d_scale_rows, 0, d_scales.rearrange("g r n -> r g n"))
-
         nc.scalar.activation(ln_wg_first[:], wg_sb[:, 0, 0:1], ACT.Ln)
         nc.scalar.activation(ln_wg[:], wg_sb[:].rearrange("p g t -> p (g t)"), ACT.Ln)
         nc.scalar.activation(warm[:], ln_wg[:, 0:1], ACT.Exp)
+        v_tab_words = keep.tile([P, T], I32, name="v_tab_words", tag="v_tab_words")
+        nc.sync.dma_start(v_tab_words[:], tab_words[0].rearrange("p t i -> p (t i)").bitcast(I32))
 
-        q_words, q_scales, v_words, v_scales_listed, w_raw, e_bf, den, num = {}, {}, {}, {}, {}, {}, {}, {}
+        q_words, v_words, v_scales_listed, w_raw, e_bf, den, num = {}, {}, {}, {}, {}, {}, {}
+        q_scales = keep.tile([P, S2], U8, name="q_scales", align_bytes=ALIGN)
         units = [(g, c) for g in range(PASSES) for c in range(CHUNKS)]
         v_scales = [keep.tile([P, PASS], U8, name="v_scales%d" % g, align_bytes=ALIGN) for g in range(PASSES)]
         e_words = {u: keep.tile([P, CHUNK], U32, name="e_words%d%d" % u, align_bytes=ALIGN) for u in units}
         e_scales = {u: keep.tile([P, CHUNK], U8, name="e_scales%d%d" % u, align_bytes=ALIGN) for u in units}
-        e_rows = {u: keep.tile([P, SLOTS, CHUNK], BF16, name="e_rows%d%d" % u) for u in units}
-        w_words = [keep.tile([P, N], U32, name="w_words%d" % g, align_bytes=ALIGN) for g in range(PASSES)]
+        e_rows = {
+            u: keep.tile([P, SLOTS, CHUNK], BF16, name="e_rows%d%d" % u, tag="e_rows%d%d" % u, align_bytes=ALIGN)
+            for u in units
+        }
+        w_words, w_bf = {}, {}
         w_scales = [keep.tile([P, N], U8, name="w_scales%d" % g, align_bytes=ALIGN) for g in range(PASSES)]
-        w_bf = [keep.tile([P, N, SLOTS], BF16, name="w_bf%d" % g, align_bytes=ALIGN) for g in range(PASSES)]
+        w_bf[0] = keep.tile([P, N, SLOTS], BF16, name="w_bf0", align_bytes=ALIGN)[:]
         scratch = {
             (n, c): keep.tile([P, CHUNK], F32, name="scratch%d%d" % (n, c))
             for n in range(N_TILES)
@@ -105,9 +103,8 @@ def tile_list_replay_kernel_control_kernel(
         def entries(k):
             return slice(k * LIST_COLS, (k + 1) * LIST_COLS)
 
-        def gather_q_scales(c):
-            q_scales[c] = keep.tile([P, CHUNK], U8, name="q_scales%d" % c, align_bytes=ALIGN)
-            nc.vector.tensor_copy(q_scales[c][:], q_tab_scales[:].bitcast(U8).indirect(q_list[:, entries(c)]))
+        def gather_q_scales():
+            nc.vector.tensor_copy(q_scales[:], q_tab_scales[:].bitcast(U8).indirect(q_list[:]))
 
         def gather_q_words(c):
             q_words[c] = keep.tile([P, CHUNK], U32, name="q_words%d" % c, tag="q_words%d" % c, align_bytes=ALIGN)
@@ -148,23 +145,26 @@ def tile_list_replay_kernel_control_kernel(
                 )
 
         def round_w(g):
-            interleave(w_bf[g][:], w_raw[g][:])
+            interleave(w_bf[g], w_raw[g][:])
 
         def quantize_w(g):
+            tag = "q_words0" if g == 0 else "w_words%d" % g
+            w_words[g] = keep.tile([P, N], U32, name="w_words%d" % g, tag=tag, align_bytes=ALIGN)
             nc.vector.quantize_mx(
-                out=w_words[g][:].bitcast(FP8X4), scales=w_scales[g][:], in_=w_bf[g][:].rearrange("p n t -> p (n t)")
+                out=w_words[g][:].bitcast(FP8X4), scales=w_scales[g][:], in_=w_bf[g].rearrange("p n t -> p (n t)")
             )
 
         def kernel_values(g, c):
             for t in range(SLOTS):
-                acc = bank(((c * PASSES + g) * SLOTS + t) % A_BANKS)
+                k = (c * PASSES + g) * SLOTS + t
+                acc = bank(k % BANKS if k < NARROW_FROM else NUM_BANKS[0][k % N_TILES])
                 m = slice(t * P, (t + 1) * P)
                 nc.tensor.matmul_mx(
                     out=acc[:],
                     lhsT=v_words[g][:, m].bitcast(FP8X4),
                     lhsT_scale=v_scales[g][V_ROW:P, m],
                     rhs=q_words[c][:].bitcast(FP8X4),
-                    rhs_scale=q_scales[c][Q_ROW:P, :],
+                    rhs_scale=q_scales[Q_ROW:P, c * CHUNK : (c + 1) * CHUNK],
                     start=True,
                     stop=True,
                 )
@@ -172,28 +172,37 @@ def tile_list_replay_kernel_control_kernel(
                 bias = ln_wg_first[:] if (g, c, t) == (0, 0, 0) else ln_wg[:, col : col + 1]
                 nc.scalar.activation(e_rows[g, c][:, t, :], acc[:], ACT.Exp, bias=bias)
 
-        def interleave_e(g, c):
+        def interleave_e(g, c, parts=1):
             e_bf[g, c] = ring.tile([P, CHUNK, SLOTS], BF16, name="e_bf", align_bytes=ALIGN)
-            interleave(e_bf[g, c][:], e_rows[g, c][:])
+            for j0 in range(0, CHUNK, CHUNK // parts):
+                j = slice(j0, j0 + CHUNK // parts)
+                interleave(e_bf[g, c][:, j, :], e_rows[g, c][:, :, j])
 
-        def quantize_e(g, c):
-            nc.vector.quantize_mx(
-                out=e_words[g, c][:].bitcast(FP8X4),
-                scales=e_scales[g, c][:],
-                in_=e_bf[g, c][:].rearrange("p j t -> p (j t)"),
-            )
+        def quantize_e(g, c, parts=1):
+            for j0 in range(0, CHUNK, CHUNK // parts):
+                j = slice(j0, j0 + CHUNK // parts)
+                nc.vector.quantize_mx(
+                    out=e_words[g, c][:, j].bitcast(FP8X4),
+                    scales=e_scales[g, c][:, j],
+                    in_=e_bf[g, c][:, j, :].rearrange("p j t -> p (j t)"),
+                )
 
         load_w(0)
-        gather_q_scales(0)
+        gather_q_scales()
+        d_scale_rows = keep.tile(
+            [P, PASSES, N // 4], I32, name="d_scale_rows", tag="d_scale_rows", align_bytes=ALIGN
+        )
+        nc.gpsimd.memset(d_scale_rows[:], 0)
+        load_scale_rows(d_scale_rows, 0, d_scales.rearrange("g r n -> r g n"))
         gather_q_words(0)
         gather_v_scales(0)
+        gather_v_scales(1)
         order_v_scales(0)
         load_w(1)
         gather_v_words(0)
-        gather_v_scales(1)
-        kernel_values(0, 0)
         order_v_scales(1)
         load_w(2)
+        kernel_values(0, 0)
         gather_v_words(1)
         gather_v_scales(2)
         kernel_values(1, 0)
@@ -202,7 +211,6 @@ def tile_list_replay_kernel_control_kernel(
         d_codes = keep.tile([P, PASSES, 2 * N // 4], I32, name="d_codes", tag="d_codes", align_bytes=ALIGN)
         nc.sync.dma_start(d_codes[:], d_words.rearrange("g p b -> p g b").bitcast(I32))
         kernel_values(2, 0)
-        gather_q_scales(1)
         gather_q_words(1)
         bn_sb = keep.tile([P, N_TILES], F32, name="bn_sb", tag="q_tab_words")
         with nc.allow_non_contiguous_dma(reason="one bias value a partition and row tile"):
@@ -210,10 +218,10 @@ def tile_list_replay_kernel_control_kernel(
         for g in range(PASSES):
             kernel_values(g, 1)
 
-        def den_passes(c, passes):
-            for n in range(N_TILES):
+        def den_passes(c, tiles, passes):
+            for n in tiles:
                 if passes[0] == 0:
-                    den[n, c] = bank(DEN_BANKS[n])
+                    den[n, c] = bank(DEN_BANKS[c][n])
                 for g in passes:
                     nc.tensor.matmul_mx(
                         out=den[n, c][:],
@@ -225,49 +233,57 @@ def tile_list_replay_kernel_control_kernel(
                         stop=(g == PASSES - 1),
                     )
 
-        def num_tile(n, c):
-            num[n, c] = bank(NUM_BANKS[n])
-            m = slice(n * P, (n + 1) * P)
-            for g in range(PASSES):
-                nc.tensor.matmul_mx(
-                    out=num[n, c][:],
-                    lhsT=w_words[g][:, m].bitcast(FP8X4),
-                    lhsT_scale=w_scales[g][:, m],
-                    rhs=e_words[g, c][:].bitcast(FP8X4),
-                    rhs_scale=e_scales[g, c][:],
-                    start=(g == 0),
-                    stop=(g == PASSES - 1),
-                )
+        def num_passes(c, tiles, passes):
+            for n in tiles:
+                if passes[0] == 0:
+                    num[n, c] = bank(NUM_BANKS[c][n])
+                m = slice(n * P, (n + 1) * P)
+                for g in passes:
+                    nc.tensor.matmul_mx(
+                        out=num[n, c][:],
+                        lhsT=w_words[g][:, m].bitcast(FP8X4),
+                        lhsT_scale=w_scales[g][:, m],
+                        rhs=e_words[g, c][:].bitcast(FP8X4),
+                        rhs_scale=e_scales[g, c][:],
+                        start=(g == 0),
+                        stop=(g == PASSES - 1),
+                    )
 
         def square_den(n, c):
             nc.scalar.activation(scratch[n, c][:], den[n, c][:], ACT.Square)
 
         round_w_on_gpsimd(0)
-        interleave_e(0, 0)
+        interleave_e(0, 0, 2)
+        quantize_e(0, 0, 2)
         interleave_e(1, 0)
-        quantize_e(0, 0)
-        interleave_e(2, 0)
+        quantize_w(0)
         quantize_e(1, 0)
-        round_w(1)
-        quantize_e(2, 0)
-        den_passes(0, [0, 1, 2])
+        interleave_e(2, 0, 2)
+        quantize_e(2, 0, 2)
+        den_passes(0, range(N_TILES), [0, 1])
+        den_passes(0, range(N_TILES), [2])
         for n in range(N_TILES):
             square_den(n, 0)
-        quantize_w(0)
+        w_bf_late = keep.tile([P, 2, N, SLOTS], BF16, name="w_bf_late", tag="e_rows20", align_bytes=ALIGN)
+        w_bf[1], w_bf[2] = w_bf_late[:, 0], w_bf_late[:, 1]
+        round_w(1)
         round_w(2)
         quantize_w(1)
+        num_passes(0, range(N_TILES), [0, 1])
         interleave_e(0, 1)
         quantize_w(2)
-        for n in range(N_TILES):
-            num_tile(n, 0)
+        num_passes(0, range(N_TILES), [2])
         interleave_e(1, 1)
         quantize_e(0, 1)
-        den_passes(1, [0])
+        den_passes(1, [0, 1], [0])
+        num_passes(1, [0, 1], [0])
         quantize_e(1, 1)
-        den_passes(1, [1])
-        interleave_e(2, 1)
-        quantize_e(2, 1)
-        den_passes(1, [2])
+        den_passes(1, [0, 1], [1])
+        num_passes(1, [0, 1], [1])
+        interleave_e(2, 1, 2)
+        quantize_e(2, 1, 2)
+        den_passes(1, [0, 1], [2])
+        num_passes(1, [0, 1], [2])
 
         recip = keep.tile([P, N_TILES * CHUNKS, CHUNK], F32, name="recip", tag="recip")
 
@@ -276,8 +292,8 @@ def tile_list_replay_kernel_control_kernel(
             radicand = den[n, c] if twice else scratch[n, c]
             ratio = keep.tile([P, CHUNK], F32, name="ratio%d%d" % (n, c))
             res = keep.tile([P, CHUNK], F32, name="res%d%d" % (n, c))
-            width = CHUNK // 2 if halved else CHUNK
-            parts = [slice(j0, j0 + width) for j0 in range(0, CHUNK, width)]
+            cuts = (0, CHUNK // 2, 3 * CHUNK // 4, CHUNK) if halved else (0, CHUNK)
+            parts = [slice(j0, j1) for j0, j1 in zip(cuts, cuts[1:])]
             for j in parts:
                 nc.scalar.activation(r[:, j], radicand[:, j], ACT.Abs_reciprocal_sqrt)
                 nc.vector.tensor_tensor(ratio[:, j], num[n, c][:, j], r[:, j], ALU.mult)
@@ -291,8 +307,12 @@ def tile_list_replay_kernel_control_kernel(
 
         for n in range(N_TILES):
             finish(n, 0, False, False)
-            num_tile(n, 1)
+            if n < 2:
+                den_passes(1, [n + 2], [0, 1, 2])
+            else:
+                num_passes(1, [n], [0, 1, 2])
         for n in range(N_TILES):
-            if n != TWICE:
-                square_den(n, 1)
-            finish(n, 1, n == TWICE, n >= HALVED)
+            if n == TWICE:
+                for later in range(TWICE, N_TILES):
+                    square_den(later, 1)
+            finish(n, 1, n < TWICE, n >= HALVED)

@@ -60,8 +60,8 @@ def tile_list_replay_kernel_control_kernel(
         v_tab_scales = keep.tile([P, T // 4], I32, name="v_tab_scales", tag="q_words1", align_bytes=ALIGN)
         q_tab_scales = keep.tile([P, T2 // 4], I32, name="q_tab_scales", tag="d_scale_rows", align_bytes=ALIGN)
         wg_sb = keep.tile([P, PASSES, SLOTS], F32, name="wg_sb", tag="v_tab_words")
-        ln_wg = keep.tile([P, PASSES * SLOTS], F32, name="ln_wg", tag="recip")
-        ln_wg_first = keep.tile([P, 1], F32, name="ln_wg_first", tag="d_codes", align_bytes=ALIGN)
+        ln_wg = keep.tile([P, PASSES * SLOTS], F32, name="ln_wg", tag="den_squares")
+        ln_wg_first = keep.tile([P, 1], F32, name="ln_wg_first", tag="w_raw2", align_bytes=ALIGN)
         warm = keep.tile([P, 1], F32, name="warm", tag="w_raw0", align_bytes=ALIGN)
 
         nc.gpsimd.memset(q_tab_scales[:], 0)
@@ -94,11 +94,7 @@ def tile_list_replay_kernel_control_kernel(
         w_words, w_bf = {}, {}
         w_scales = [keep.tile([P, N], U8, name="w_scales%d" % g, align_bytes=ALIGN) for g in range(PASSES)]
         w_bf[0] = keep.tile([P, N, SLOTS], BF16, name="w_bf0", align_bytes=ALIGN)[:]
-        scratch = {
-            (n, c): keep.tile([P, CHUNK], F32, name="scratch%d%d" % (n, c))
-            for n in range(N_TILES)
-            for c in range(CHUNKS)
-        }
+        scratch = {(n, 1): keep.tile([P, CHUNK], F32, name="scratch%d" % n)[:] for n in range(N_TILES)}
 
         def entries(k):
             return slice(k * LIST_COLS, (k + 1) * LIST_COLS)
@@ -111,7 +107,7 @@ def tile_list_replay_kernel_control_kernel(
             nc.vector.tensor_copy(q_words[c][:], q_tab_words[:].bitcast(U32).indirect(q_list[:, entries(c)]))
 
         def gather_v_scales(g):
-            tag = ("w_raw1", "w_raw2", "d_codes")[g]
+            tag = ("w_raw1", "d_codes", "w_raw2")[g]
             v_scales_listed[g] = keep.tile([P, PASS], U8, name="v_scales_listed%d" % g, tag=tag, align_bytes=ALIGN)
             nc.vector.tensor_copy(v_scales_listed[g][:], v_tab_scales[:].bitcast(U8).indirect(v_list[:, entries(g)]))
 
@@ -201,22 +197,21 @@ def tile_list_replay_kernel_control_kernel(
         load_w(1)
         gather_v_words(0)
         order_v_scales(1)
-        load_w(2)
+        d_codes = keep.tile([P, PASSES, 2 * N // 4], I32, name="d_codes", tag="d_codes", align_bytes=ALIGN)
+        nc.sync.dma_start(d_codes[:], d_words.rearrange("g p b -> p g b").bitcast(I32))
         kernel_values(0, 0)
         gather_v_words(1)
         gather_v_scales(2)
         kernel_values(1, 0)
         gather_v_words(2)
         order_v_scales(2)
-        d_codes = keep.tile([P, PASSES, 2 * N // 4], I32, name="d_codes", tag="d_codes", align_bytes=ALIGN)
-        nc.sync.dma_start(d_codes[:], d_words.rearrange("g p b -> p g b").bitcast(I32))
+        load_w(2)
         kernel_values(2, 0)
         gather_q_words(1)
         bn_sb = keep.tile([P, N_TILES], F32, name="bn_sb", tag="q_tab_words")
         with nc.allow_non_contiguous_dma(reason="one bias value a partition and row tile"):
             nc.sync.dma_start(bn_sb[:], bn.rearrange("(n p) -> p n", p=P))
-        for g in range(PASSES):
-            kernel_values(g, 1)
+        kernel_values(0, 1)
 
         def den_passes(c, tiles, passes):
             for n in tiles:
@@ -250,26 +245,32 @@ def tile_list_replay_kernel_control_kernel(
                     )
 
         def square_den(n, c):
-            nc.scalar.activation(scratch[n, c][:], den[n, c][:], ACT.Square)
+            nc.scalar.activation(scratch[n, c], den[n, c][:], ACT.Square)
 
         round_w_on_gpsimd(0)
         interleave_e(0, 0, 2)
         quantize_e(0, 0, 2)
+        den_passes(0, range(N_TILES), [0])
+        kernel_values(1, 1)
         interleave_e(1, 0)
         quantize_w(0)
         quantize_e(1, 0)
+        den_passes(0, range(N_TILES), [1])
+        kernel_values(2, 1)
         interleave_e(2, 0, 2)
         quantize_e(2, 0, 2)
-        den_passes(0, range(N_TILES), [0, 1])
         den_passes(0, range(N_TILES), [2])
+        den_squares = keep.tile([P, N_TILES, CHUNK], F32, name="den_squares", tag="den_squares")
         for n in range(N_TILES):
+            scratch[n, 0] = den_squares[:, n, :]
             square_den(n, 0)
         w_bf_late = keep.tile([P, 2, N, SLOTS], BF16, name="w_bf_late", tag="e_rows20", align_bytes=ALIGN)
         w_bf[1], w_bf[2] = w_bf_late[:, 0], w_bf_late[:, 1]
+        num_passes(0, range(N_TILES), [0])
         round_w(1)
         round_w(2)
         quantize_w(1)
-        num_passes(0, range(N_TILES), [0, 1])
+        num_passes(0, range(N_TILES), [1])
         interleave_e(0, 1)
         quantize_w(2)
         num_passes(0, range(N_TILES), [2])
@@ -285,34 +286,56 @@ def tile_list_replay_kernel_control_kernel(
         den_passes(1, [0, 1], [2])
         num_passes(1, [0, 1], [2])
 
-        recip = keep.tile([P, N_TILES * CHUNKS, CHUNK], F32, name="recip", tag="recip")
+        recip = keep.tile([P, N_TILES * CHUNKS, CHUNK], F32, name="recip")
 
-        def finish(n, c, twice, halved):
-            r = recip[:, c * N_TILES + n, :]
-            radicand = den[n, c] if twice else scratch[n, c]
-            ratio = keep.tile([P, CHUNK], F32, name="ratio%d%d" % (n, c))
-            res = keep.tile([P, CHUNK], F32, name="res%d%d" % (n, c))
+        ratios, cut = {}, {}
+
+        def inverse(n, c, twice, halved):
             cuts = (0, CHUNK // 2, 3 * CHUNK // 4, CHUNK) if halved else (0, CHUNK)
-            parts = [slice(j0, j1) for j0, j1 in zip(cuts, cuts[1:])]
-            for j in parts:
-                nc.scalar.activation(r[:, j], radicand[:, j], ACT.Abs_reciprocal_sqrt)
+            cut[n, c] = [slice(j0, j1) for j0, j1 in zip(cuts, cuts[1:])]
+            radicand = den[n, c] if twice else scratch[n, c]
+            for j in cut[n, c]:
+                nc.scalar.activation(recip[:, c * N_TILES + n, j], radicand[:, j], ACT.Abs_reciprocal_sqrt)
+
+        def divide(n, c, twice):
+            r = recip[:, c * N_TILES + n, :]
+            ratio = keep.tile([P, CHUNK], F32, name="ratio%d%d" % (n, c))
+            for j in cut[n, c]:
                 nc.vector.tensor_tensor(ratio[:, j], num[n, c][:, j], r[:, j], ALU.mult)
             if twice:
-                nc.vector.tensor_tensor(scratch[n, c][:], ratio[:], r, ALU.mult)
+                nc.vector.tensor_tensor(scratch[n, c], ratio[:], r, ALU.mult)
                 ratio = scratch[n, c]
-            adder = nc.vector if halved else nc.gpsimd
-            for j in parts:
-                adder.tensor_scalar(res[:, j], ratio[:, j], 1.0, bn_sb[:, n : n + 1], ALU.mult, ALU.add)
+            ratios[n, c] = ratio
+
+        def add_bias_and_store(n, c, engine):
+            res = keep.tile([P, CHUNK], F32, name="res%d%d" % (n, c))
+            bias = bn_sb[:, n : n + 1]
+            for j in cut[n, c]:
+                if engine == "scalar":
+                    nc.scalar.activation(res[:, j], ratios[n, c][:, j], ACT.Identity, bias=bias)
+                else:
+                    adder = nc.vector if engine == "vector" else nc.gpsimd
+                    adder.tensor_scalar(res[:, j], ratios[n, c][:, j], 1.0, bias, ALU.mult, ALU.add)
                 nc.sync.dma_start(out[n * P : (n + 1) * P, c * CHUNK + j.start : c * CHUNK + j.stop], res[:, j])
 
+        def finish(n, c, twice):
+            inverse(n, c, twice, False)
+            divide(n, c, twice)
+            add_bias_and_store(n, c, "gpsimd")
+
         for n in range(N_TILES):
-            finish(n, 0, False, False)
+            finish(n, 0, False)
             if n < 2:
                 den_passes(1, [n + 2], [0, 1, 2])
             else:
                 num_passes(1, [n], [0, 1, 2])
-        for n in range(N_TILES):
-            if n == TWICE:
-                for later in range(TWICE, N_TILES):
-                    square_den(later, 1)
-            finish(n, 1, n < TWICE, n >= HALVED)
+        for n in range(TWICE):
+            finish(n, 1, True)
+        for n in range(TWICE, N_TILES):
+            square_den(n, 1)
+        inverse(2, 1, False, False)
+        divide(2, 1, False)
+        inverse(3, 1, False, True)
+        add_bias_and_store(2, 1, "scalar")
+        divide(3, 1, False)
+        add_bias_and_store(3, 1, "vector")

@@ -27,15 +27,16 @@ LIST_COLS = PASS // 16
 RUN = 4
 ALIGN = 64
 
+V_FIRST = 3 * T // 16
 V_ROW = 8
 Q_ROW = 4
 
 BANKS = 8
-NARROW_FROM = 8
-NUM_BANKS = ((0, 1, 2, 3), (5, 7, 2, 3))
-DEN_BANKS = ((4, 5, 6, 7), (4, 6, 0, 1))
+NARROW_FROM = 16
+NUM_BANKS = ((0, 1, 2, 3), (0, 1, 2, 3))
+DEN_BANKS = ((0, 1, 2, 3), (4, 5, 6, 7))
 
-TWICE = 2
+TWICE = 1
 HALVED = 3
 
 
@@ -57,32 +58,41 @@ def tile_list_replay_kernel_control_kernel(
 
         v_list = keep.tile([P, S // 16], U16, name="v_list")
         q_list = keep.tile([P, S2 // 16], U16, name="q_list")
-        v_tab_scales = keep.tile([P, T // 4], I32, name="v_tab_scales", tag="q_words1", align_bytes=ALIGN)
-        q_tab_scales = keep.tile([P, T2 // 4], I32, name="q_tab_scales", tag="d_scale_rows", align_bytes=ALIGN)
-        wg_sb = keep.tile([P, PASSES, SLOTS], F32, name="wg_sb", tag="v_tab_words")
-        ln_wg = keep.tile([P, PASSES * SLOTS], F32, name="ln_wg", tag="den_squares")
-        ln_wg_first = keep.tile([P, 1], F32, name="ln_wg_first", tag="w_raw2", align_bytes=ALIGN)
-        warm = keep.tile([P, 1], F32, name="warm", tag="w_raw0", align_bytes=ALIGN)
+        v_tab_scales = keep.tile([P, T // 4], I32, name="v_tab_scales", tag="d_scale_rows", align_bytes=ALIGN)
+        q_tab_scales = keep.tile([P, T2 // 4], I32, name="q_tab_scales", align_bytes=ALIGN)
+        wg_sb = keep.tile([P, PASSES, SLOTS], F32, name="wg_sb")
+        ln_wg = keep.tile([P, PASSES * SLOTS], F32, name="ln_wg", tag="recip")
+        gate_tags = ("v_words1", "v_words2", "q_scales1")
+        ln_first = [
+            keep.tile([P, 1], F32, name="ln_first%d" % t, tag=gate_tags[t], align_bytes=ALIGN) for t in range(3)
+        ]
+        ln_late = keep.tile([P, SLOTS], F32, name="ln_late", tag="den_squares")
+        warm = keep.tile([P, 1], F32, name="warm", tag="w_raw2", align_bytes=ALIGN)
 
+        nc.gpsimd.memset(v_tab_scales[:, : T // 8], 0)
+        nc.vector.memset(v_tab_scales[:, T // 8 :], 0)
         nc.gpsimd.memset(q_tab_scales[:], 0)
-        nc.vector.memset(v_tab_scales[:], 0)
 
-        nc.sync.dma_start(q_list[:], offs2)
+        v_tab_words = keep.tile([P, T], I32, name="v_tab_words")
+        q_tab_words = keep.tile([P, T2], I32, name="q_tab_words", tag="q_tab_words")
+        v_words_hbm = tab_words[0].rearrange("p t i -> p (t i)").bitcast(I32)
         nc.sync.dma_start(v_list[:], offs)
+        nc.sync.dma_start(v_tab_words[:, :V_FIRST], v_words_hbm[:, :V_FIRST])
+        nc.sync.dma_start(q_list[:], offs2)
+        load_scale_rows(v_tab_scales, V_ROW, tab_scales[0])
+        nc.sync.dma_start(v_tab_words[:, V_FIRST:], v_words_hbm[:, V_FIRST:])
         nc.sync.dma_start(wg_sb[:], wg.rearrange("(g p t) -> p g t", p=P, t=SLOTS))
         load_scale_rows(q_tab_scales, Q_ROW, tab2_scales[0])
-        q_tab_words = keep.tile([P, T2], I32, name="q_tab_words", tag="q_tab_words")
         nc.sync.dma_start(q_tab_words[:], tab2_words[0].rearrange("p t i -> p (t i)").bitcast(I32))
-        load_scale_rows(v_tab_scales, V_ROW, tab_scales[0])
 
-        nc.scalar.activation(ln_wg_first[:], wg_sb[:, 0, 0:1], ACT.Ln)
         nc.scalar.activation(ln_wg[:], wg_sb[:].rearrange("p g t -> p (g t)"), ACT.Ln)
+        for t in range(3):
+            nc.scalar.copy(ln_first[t][:], ln_wg[:, t : t + 1])
+        nc.scalar.copy(ln_late[:], ln_wg[:, SLOTS : 2 * SLOTS])
         nc.scalar.activation(warm[:], ln_wg[:, 0:1], ACT.Exp)
-        v_tab_words = keep.tile([P, T], I32, name="v_tab_words", tag="v_tab_words")
-        nc.sync.dma_start(v_tab_words[:], tab_words[0].rearrange("p t i -> p (t i)").bitcast(I32))
 
         q_words, v_words, v_scales_listed, w_raw, e_bf, den, num = {}, {}, {}, {}, {}, {}, {}
-        q_scales = keep.tile([P, S2], U8, name="q_scales", align_bytes=ALIGN)
+        q_scales = {}
         units = [(g, c) for g in range(PASSES) for c in range(CHUNKS)]
         v_scales = [keep.tile([P, PASS], U8, name="v_scales%d" % g, align_bytes=ALIGN) for g in range(PASSES)]
         e_words = {u: keep.tile([P, CHUNK], U32, name="e_words%d%d" % u, align_bytes=ALIGN) for u in units}
@@ -99,15 +109,20 @@ def tile_list_replay_kernel_control_kernel(
         def entries(k):
             return slice(k * LIST_COLS, (k + 1) * LIST_COLS)
 
-        def gather_q_scales():
-            nc.vector.tensor_copy(q_scales[:], q_tab_scales[:].bitcast(U8).indirect(q_list[:]))
+        def gather_q_scales(c):
+            q_scales[c] = keep.tile([P, CHUNK], U8, name="q_scales%d" % c, tag="q_scales%d" % c, align_bytes=ALIGN)
+            nc.vector.tensor_copy(q_scales[c][:], q_tab_scales[:].bitcast(U8).indirect(q_list[:, entries(c)]))
 
         def gather_q_words(c):
             q_words[c] = keep.tile([P, CHUNK], U32, name="q_words%d" % c, tag="q_words%d" % c, align_bytes=ALIGN)
-            nc.vector.tensor_copy(q_words[c][:], q_tab_words[:].bitcast(U32).indirect(q_list[:, entries(c)]))
+            parts = 2 if c == 0 else 1
+            for h in range(parts):
+                j = slice(h * CHUNK // parts, (h + 1) * CHUNK // parts)
+                cols = slice(c * LIST_COLS + j.start // 16, c * LIST_COLS + j.stop // 16)
+                nc.vector.tensor_copy(q_words[c][:, j], q_tab_words[:].bitcast(U32).indirect(q_list[:, cols]))
 
         def gather_v_scales(g):
-            tag = ("w_raw1", "d_codes", "w_raw2")[g]
+            tag = ("w_raw0", "w_raw1", "d_codes")[g]
             v_scales_listed[g] = keep.tile([P, PASS], U8, name="v_scales_listed%d" % g, tag=tag, align_bytes=ALIGN)
             nc.vector.tensor_copy(v_scales_listed[g][:], v_tab_scales[:].bitcast(U8).indirect(v_list[:, entries(g)]))
 
@@ -118,7 +133,7 @@ def tile_list_replay_kernel_control_kernel(
             )
 
         def gather_v_words(g):
-            v_words[g] = keep.tile([P, PASS], U32, name="v_words%d" % g, align_bytes=ALIGN)
+            v_words[g] = keep.tile([P, PASS], U32, name="v_words%d" % g, tag="v_words%d" % g, align_bytes=ALIGN)
             nc.vector.tensor_copy(
                 v_words[g][:].rearrange("p (t m) -> p m t", t=SLOTS),
                 v_tab_words[:].bitcast(U32).indirect(v_list[:, entries(g)]),
@@ -150,23 +165,26 @@ def tile_list_replay_kernel_control_kernel(
                 out=w_words[g][:].bitcast(FP8X4), scales=w_scales[g][:], in_=w_bf[g].rearrange("p n t -> p (n t)")
             )
 
-        def kernel_values(g, c):
+        def kernel_values(g, c, first_bank, j=slice(0, CHUNK)):
             for t in range(SLOTS):
-                k = (c * PASSES + g) * SLOTS + t
-                acc = bank(k % BANKS if k < NARROW_FROM else NUM_BANKS[0][k % N_TILES])
+                acc = bank(first_bank + t)
                 m = slice(t * P, (t + 1) * P)
                 nc.tensor.matmul_mx(
-                    out=acc[:],
+                    out=acc[:, j],
                     lhsT=v_words[g][:, m].bitcast(FP8X4),
                     lhsT_scale=v_scales[g][V_ROW:P, m],
-                    rhs=q_words[c][:].bitcast(FP8X4),
-                    rhs_scale=q_scales[Q_ROW:P, c * CHUNK : (c + 1) * CHUNK],
+                    rhs=q_words[c][:, j].bitcast(FP8X4),
+                    rhs_scale=q_scales[c][Q_ROW:P, j],
                     start=True,
                     stop=True,
                 )
                 col = g * SLOTS + t
-                bias = ln_wg_first[:] if (g, c, t) == (0, 0, 0) else ln_wg[:, col : col + 1]
-                nc.scalar.activation(e_rows[g, c][:, t, :], acc[:], ACT.Exp, bias=bias)
+                bias = ln_wg[:, col : col + 1]
+                if (g, c, j.start) == (0, 0, 0) and t < 3:
+                    bias = ln_first[t][:]
+                if (g, c) == (1, 1):
+                    bias = ln_late[:, t : t + 1]
+                nc.scalar.activation(e_rows[g, c][:, t, j], acc[:, j], ACT.Exp, bias=bias)
 
         def interleave_e(g, c, parts=1):
             e_bf[g, c] = ring.tile([P, CHUNK, SLOTS], BF16, name="e_bf", align_bytes=ALIGN)
@@ -183,35 +201,37 @@ def tile_list_replay_kernel_control_kernel(
                     in_=e_bf[g, c][:, j, :].rearrange("p j t -> p (j t)"),
                 )
 
+        gather_v_scales(0)
+        gather_v_scales(1)
+        order_v_scales(0)
         load_w(0)
-        gather_q_scales()
+        gather_v_scales(2)
+        order_v_scales(1)
+        load_w(1)
+        order_v_scales(2)
+        d_codes = keep.tile([P, PASSES, 2 * N // 4], I32, name="d_codes", tag="d_codes", align_bytes=ALIGN)
+        nc.sync.dma_start(d_codes[:], d_words.rearrange("g p b -> p g b").bitcast(I32))
         d_scale_rows = keep.tile(
             [P, PASSES, N // 4], I32, name="d_scale_rows", tag="d_scale_rows", align_bytes=ALIGN
         )
         nc.gpsimd.memset(d_scale_rows[:], 0)
         load_scale_rows(d_scale_rows, 0, d_scales.rearrange("g r n -> r g n"))
-        gather_q_words(0)
-        gather_v_scales(0)
-        gather_v_scales(1)
-        order_v_scales(0)
-        load_w(1)
-        gather_v_words(0)
-        order_v_scales(1)
-        d_codes = keep.tile([P, PASSES, 2 * N // 4], I32, name="d_codes", tag="d_codes", align_bytes=ALIGN)
-        nc.sync.dma_start(d_codes[:], d_words.rearrange("g p b -> p g b").bitcast(I32))
-        kernel_values(0, 0)
-        gather_v_words(1)
-        gather_v_scales(2)
-        kernel_values(1, 0)
-        gather_v_words(2)
-        order_v_scales(2)
         load_w(2)
-        kernel_values(2, 0)
+        gather_v_words(0)
+        gather_q_scales(0)
+        gather_q_words(0)
         gather_q_words(1)
+        kernel_values(0, 0, 0, slice(0, CHUNK // 2))
+        kernel_values(0, 0, 4, slice(CHUNK // 2, CHUNK))
+        gather_v_words(1)
+        gather_v_words(2)
+        gather_q_scales(1)
+        kernel_values(1, 0, 0)
+        kernel_values(2, 0, 4)
         bn_sb = keep.tile([P, N_TILES], F32, name="bn_sb", tag="q_tab_words")
         with nc.allow_non_contiguous_dma(reason="one bias value a partition and row tile"):
             nc.sync.dma_start(bn_sb[:], bn.rearrange("(n p) -> p n", p=P))
-        kernel_values(0, 1)
+        kernel_values(0, 1, 0)
 
         def den_passes(c, tiles, passes):
             for n in tiles:
@@ -251,12 +271,11 @@ def tile_list_replay_kernel_control_kernel(
         interleave_e(0, 0, 2)
         quantize_e(0, 0, 2)
         den_passes(0, range(N_TILES), [0])
-        kernel_values(1, 1)
         interleave_e(1, 0)
         quantize_w(0)
         quantize_e(1, 0)
         den_passes(0, range(N_TILES), [1])
-        kernel_values(2, 1)
+        kernel_values(1, 1, 4)
         interleave_e(2, 0, 2)
         quantize_e(2, 0, 2)
         den_passes(0, range(N_TILES), [2])
@@ -264,6 +283,7 @@ def tile_list_replay_kernel_control_kernel(
         for n in range(N_TILES):
             scratch[n, 0] = den_squares[:, n, :]
             square_den(n, 0)
+        kernel_values(2, 1, 4)
         w_bf_late = keep.tile([P, 2, N, SLOTS], BF16, name="w_bf_late", tag="e_rows20", align_bytes=ALIGN)
         w_bf[1], w_bf[2] = w_bf_late[:, 0], w_bf_late[:, 1]
         num_passes(0, range(N_TILES), [0])
@@ -276,17 +296,14 @@ def tile_list_replay_kernel_control_kernel(
         num_passes(0, range(N_TILES), [2])
         interleave_e(1, 1)
         quantize_e(0, 1)
-        den_passes(1, [0, 1], [0])
-        num_passes(1, [0, 1], [0])
+        den_passes(1, range(N_TILES), [0])
         quantize_e(1, 1)
-        den_passes(1, [0, 1], [1])
-        num_passes(1, [0, 1], [1])
+        den_passes(1, range(N_TILES), [1])
         interleave_e(2, 1, 2)
         quantize_e(2, 1, 2)
-        den_passes(1, [0, 1], [2])
-        num_passes(1, [0, 1], [2])
+        den_passes(1, range(N_TILES), [2])
 
-        recip = keep.tile([P, N_TILES * CHUNKS, CHUNK], F32, name="recip")
+        recip = keep.tile([P, N_TILES * CHUNKS, CHUNK], F32, name="recip", tag="recip")
 
         ratios, cut = {}, {}
 
@@ -325,14 +342,13 @@ def tile_list_replay_kernel_control_kernel(
 
         for n in range(N_TILES):
             finish(n, 0, False)
-            if n < 2:
-                den_passes(1, [n + 2], [0, 1, 2])
-            else:
-                num_passes(1, [n], [0, 1, 2])
-        for n in range(TWICE):
-            finish(n, 1, True)
-        for n in range(TWICE, N_TILES):
-            square_den(n, 1)
+            num_passes(1, [n], [0, 1, 2])
+        square_den(0, 1)
+        square_den(1, 1)
+        finish(0, 1, False)
+        finish(1, 1, False)
+        square_den(2, 1)
+        square_den(3, 1)
         inverse(2, 1, False, False)
         divide(2, 1, False)
         inverse(3, 1, False, True)

@@ -52,49 +52,56 @@ def tile_list_replay_kernel_control_kernel(
         def bank(b):
             return psum.tile([P, CHUNK], F32, name="bank%d" % b, tag="bank%d" % b)
 
-        def load_scale_rows(dst, first_row, rows):
-            for r in range(4):
+        def load_scale_rows(dst, first_row, rows, which=range(4)):
+            for r in which:
                 nc.sync.dma_start(dst[first_row + r : P : 32], rows[r:16:4].bitcast(I32))
 
         v_list = keep.tile([P, S // 16], U16, name="v_list")
         q_list = keep.tile([P, S2 // 16], U16, name="q_list")
-        v_tab_scales = keep.tile([P, T // 4], I32, name="v_tab_scales", tag="d_scale_rows", align_bytes=ALIGN)
+        v_tab_scales = keep.tile([P, T // 4], I32, name="v_tab_scales", align_bytes=ALIGN)
         q_tab_scales = keep.tile([P, T2 // 4], I32, name="q_tab_scales", align_bytes=ALIGN)
+        v_scales = keep.tile([P, S // 4], I32, name="v_scales", align_bytes=ALIGN)
         wg_sb = keep.tile([P, PASSES, SLOTS], F32, name="wg_sb")
         ln_wg = keep.tile([P, PASSES * SLOTS], F32, name="ln_wg", tag="recip")
-        gate_tags = ("v_words1", "v_words2", "q_scales1")
+        gate_tags = ("v_words1", "v_words2", "q_scales1", "w_raw2")
         ln_first = [
-            keep.tile([P, 1], F32, name="ln_first%d" % t, tag=gate_tags[t], align_bytes=ALIGN) for t in range(3)
+            keep.tile([P, 1], F32, name="ln_first%d" % k, tag=tag, align_bytes=ALIGN) for k, tag in enumerate(gate_tags)
         ]
         ln_late = keep.tile([P, SLOTS], F32, name="ln_late", tag="den_squares")
-        warm = keep.tile([P, 1], F32, name="warm", tag="w_raw2", align_bytes=ALIGN)
+        warm = keep.tile([P, 1], F32, name="warm")
 
         nc.gpsimd.memset(v_tab_scales[:, : T // 8], 0)
         nc.vector.memset(v_tab_scales[:, T // 8 :], 0)
         nc.gpsimd.memset(q_tab_scales[:], 0)
+        nc.gpsimd.memset(v_scales[:], 0)
+        d_scale_rows = keep.tile([P, PASSES, N // 4], I32, name="d_scale_rows", align_bytes=ALIGN)
+        nc.gpsimd.memset(d_scale_rows[:], 0)
 
-        v_tab_words = keep.tile([P, T], I32, name="v_tab_words")
-        q_tab_words = keep.tile([P, T2], I32, name="q_tab_words", tag="q_tab_words")
+        v_tab_words = keep.tile([P, T], I32, name="v_tab_words", tag="v_tab_words")
+        q_tab_words = keep.tile([P, T2], I32, name="q_tab_words", tag="w_raw1", align_bytes=ALIGN)
         v_words_hbm = tab_words[0].rearrange("p t i -> p (t i)").bitcast(I32)
         nc.sync.dma_start(v_list[:], offs)
-        nc.sync.dma_start(v_tab_words[:, :V_FIRST], v_words_hbm[:, :V_FIRST])
-        nc.sync.dma_start(q_list[:], offs2)
-        load_scale_rows(v_tab_scales, V_ROW, tab_scales[0])
-        nc.sync.dma_start(v_tab_words[:, V_FIRST:], v_words_hbm[:, V_FIRST:])
         nc.sync.dma_start(wg_sb[:], wg.rearrange("(g p t) -> p g t", p=P, t=SLOTS))
-        load_scale_rows(q_tab_scales, Q_ROW, tab2_scales[0])
+        nc.sync.dma_start(v_tab_words[:, :V_FIRST], v_words_hbm[:, :V_FIRST])
+        nc.sync.dma_start(v_tab_scales[0:P:8], tab_scales[0].bitcast(I32))
+        nc.sync.dma_start(q_list[:], offs2)
+        load_scale_rows(q_tab_scales, Q_ROW, tab2_scales[0], range(2))
+        nc.sync.dma_start(v_tab_words[:, V_FIRST:], v_words_hbm[:, V_FIRST:])
+        load_scale_rows(q_tab_scales, Q_ROW, tab2_scales[0], range(2, 4))
         nc.sync.dma_start(q_tab_words[:], tab2_words[0].rearrange("p t i -> p (t i)").bitcast(I32))
+        d_codes = keep.tile([P, PASSES, 2 * N // 4], I32, name="d_codes", align_bytes=ALIGN)
+        nc.sync.dma_start(d_codes[:], d_words.rearrange("g p b -> p g b").bitcast(I32))
+        load_scale_rows(d_scale_rows, 0, d_scales.rearrange("g r n -> r g n"))
 
         nc.scalar.activation(ln_wg[:], wg_sb[:].rearrange("p g t -> p (g t)"), ACT.Ln)
-        for t in range(3):
-            nc.scalar.copy(ln_first[t][:], ln_wg[:, t : t + 1])
+        for k in range(len(gate_tags)):
+            nc.scalar.copy(ln_first[k][:], ln_wg[:, k % SLOTS : k % SLOTS + 1])
         nc.scalar.copy(ln_late[:], ln_wg[:, SLOTS : 2 * SLOTS])
         nc.scalar.activation(warm[:], ln_wg[:, 0:1], ACT.Exp)
 
         q_words, v_words, v_scales_listed, w_raw, e_bf, den, num = {}, {}, {}, {}, {}, {}, {}
         q_scales = {}
         units = [(g, c) for g in range(PASSES) for c in range(CHUNKS)]
-        v_scales = [keep.tile([P, PASS], U8, name="v_scales%d" % g, align_bytes=ALIGN) for g in range(PASSES)]
         e_words = {u: keep.tile([P, CHUNK], U32, name="e_words%d%d" % u, align_bytes=ALIGN) for u in units}
         e_scales = {u: keep.tile([P, CHUNK], U8, name="e_scales%d%d" % u, align_bytes=ALIGN) for u in units}
         e_rows = {
@@ -121,16 +128,20 @@ def tile_list_replay_kernel_control_kernel(
                 cols = slice(c * LIST_COLS + j.start // 16, c * LIST_COLS + j.stop // 16)
                 nc.vector.tensor_copy(q_words[c][:, j], q_tab_words[:].bitcast(U32).indirect(q_list[:, cols]))
 
-        def gather_v_scales(g):
-            tag = ("w_raw0", "w_raw1", "d_codes")[g]
-            v_scales_listed[g] = keep.tile([P, PASS], U8, name="v_scales_listed%d" % g, tag=tag, align_bytes=ALIGN)
-            nc.vector.tensor_copy(v_scales_listed[g][:], v_tab_scales[:].bitcast(U8).indirect(v_list[:, entries(g)]))
-
-        def order_v_scales(g):
-            nc.vector.tensor_copy(
-                v_scales[g][:].rearrange("p (t m) -> p t m", t=SLOTS),
-                v_scales_listed[g][:].rearrange("p (m t) -> p t m", t=SLOTS),
-            )
+        def v_scale_plane():
+            listed = keep.tile([P, S], U8, name="v_scales_listed", align_bytes=ALIGN)
+            ordered = keep.tile([P, S], U8, name="v_scales_ordered", tag="w_raw0", align_bytes=ALIGN)
+            for g in range(PASSES):
+                i = slice(g * PASS, (g + 1) * PASS)
+                nc.vector.tensor_copy(listed[:, i], v_tab_scales[:].bitcast(U8).indirect(v_list[:, entries(g)]))
+            for g in range(PASSES):
+                i = slice(g * PASS, (g + 1) * PASS)
+                nc.vector.tensor_copy(
+                    ordered[:, i].rearrange("p (t m) -> p t m", t=SLOTS),
+                    listed[:, i].rearrange("p (m t) -> p t m", t=SLOTS),
+                )
+            for r in range(4):
+                nc.scalar.dma_start(v_scales[V_ROW + r : P : 32], ordered[8 * r : P : 32].bitcast(I32))
 
         def gather_v_words(g):
             v_words[g] = keep.tile([P, PASS], U32, name="v_words%d" % g, tag="v_words%d" % g, align_bytes=ALIGN)
@@ -172,7 +183,7 @@ def tile_list_replay_kernel_control_kernel(
                 nc.tensor.matmul_mx(
                     out=acc[:, j],
                     lhsT=v_words[g][:, m].bitcast(FP8X4),
-                    lhsT_scale=v_scales[g][V_ROW:P, m],
+                    lhsT_scale=v_scales[V_ROW:P].bitcast(U8)[:, g * PASS + t * P : g * PASS + (t + 1) * P],
                     rhs=q_words[c][:, j].bitcast(FP8X4),
                     rhs_scale=q_scales[c][Q_ROW:P, j],
                     start=True,
@@ -180,8 +191,8 @@ def tile_list_replay_kernel_control_kernel(
                 )
                 col = g * SLOTS + t
                 bias = ln_wg[:, col : col + 1]
-                if (g, c, j.start) == (0, 0, 0) and t < 3:
-                    bias = ln_first[t][:]
+                if (g, c) == (0, 0) and first_bank + t < len(ln_first):
+                    bias = ln_first[first_bank + t][:]
                 if (g, c) == (1, 1):
                     bias = ln_late[:, t : t + 1]
                 nc.scalar.activation(e_rows[g, c][:, t, j], acc[:, j], ACT.Exp, bias=bias)
@@ -201,34 +212,22 @@ def tile_list_replay_kernel_control_kernel(
                     in_=e_bf[g, c][:, j, :].rearrange("p j t -> p (j t)"),
                 )
 
-        gather_v_scales(0)
-        gather_v_scales(1)
-        order_v_scales(0)
+        v_scale_plane()
         load_w(0)
-        gather_v_scales(2)
-        order_v_scales(1)
-        load_w(1)
-        order_v_scales(2)
-        d_codes = keep.tile([P, PASSES, 2 * N // 4], I32, name="d_codes", tag="d_codes", align_bytes=ALIGN)
-        nc.sync.dma_start(d_codes[:], d_words.rearrange("g p b -> p g b").bitcast(I32))
-        d_scale_rows = keep.tile(
-            [P, PASSES, N // 4], I32, name="d_scale_rows", tag="d_scale_rows", align_bytes=ALIGN
-        )
-        nc.gpsimd.memset(d_scale_rows[:], 0)
-        load_scale_rows(d_scale_rows, 0, d_scales.rearrange("g r n -> r g n"))
-        load_w(2)
-        gather_v_words(0)
         gather_q_scales(0)
+        gather_v_words(0)
         gather_q_words(0)
         gather_q_words(1)
+        load_w(1)
         kernel_values(0, 0, 0, slice(0, CHUNK // 2))
         kernel_values(0, 0, 4, slice(CHUNK // 2, CHUNK))
         gather_v_words(1)
         gather_v_words(2)
         gather_q_scales(1)
+        load_w(2)
         kernel_values(1, 0, 0)
         kernel_values(2, 0, 4)
-        bn_sb = keep.tile([P, N_TILES], F32, name="bn_sb", tag="q_tab_words")
+        bn_sb = keep.tile([P, N_TILES], F32, name="bn_sb", tag="v_tab_words")
         with nc.allow_non_contiguous_dma(reason="one bias value a partition and row tile"):
             nc.sync.dma_start(bn_sb[:], bn.rearrange("(n p) -> p n", p=P))
         kernel_values(0, 1, 0)

@@ -34,7 +34,7 @@ Q_ROW = 4
 BANKS = 8
 NARROW_FROM = 16
 NUM_BANKS = ((0, 1, 2, 3), (0, 1, 2, 3))
-DEN_BANKS = ((0, 1, 2, 3), (4, 5, 6, 7))
+DEN_BANKS = ((4, 5, 6, 7), (4, 5, 6, 7))
 
 TWICE = 1
 HALVED = 3
@@ -60,43 +60,39 @@ def tile_list_replay_kernel_control_kernel(
         q_list = keep.tile([P, S2 // 16], U16, name="q_list")
         v_tab_scales = keep.tile([P, T // 4], I32, name="v_tab_scales", align_bytes=ALIGN)
         q_tab_scales = keep.tile([P, T2 // 4], I32, name="q_tab_scales", align_bytes=ALIGN)
-        v_scales = keep.tile([P, S // 4], I32, name="v_scales", align_bytes=ALIGN)
+        planes = [
+            keep.tile([P, cols // 4], I32, name="planes%d" % k, align_bytes=ALIGN)
+            for k, cols in enumerate((2 * PASS, 2 * PASS, CHUNK))
+        ]
+        d_scale_rows = keep.tile([P, PASSES, N // 4], I32, name="d_scale_rows", align_bytes=ALIGN)
         wg_sb = keep.tile([P, PASSES, SLOTS], F32, name="wg_sb")
-        ln_wg = keep.tile([P, PASSES * SLOTS], F32, name="ln_wg", tag="recip")
-        gate_tags = ("v_words1", "v_words2", "q_scales1", "w_raw2")
+        ln_wg = keep.tile([P, PASSES * SLOTS], F32, name="ln_wg", tag="den_squares")
+        gate_tags = ("v_words1", "q_scales1", "v_words2", "w_raw2")
         ln_first = [
             keep.tile([P, 1], F32, name="ln_first%d" % k, tag=tag, align_bytes=ALIGN) for k, tag in enumerate(gate_tags)
         ]
-        ln_late = keep.tile([P, SLOTS], F32, name="ln_late", tag="den_squares")
         warm = keep.tile([P, 1], F32, name="warm")
 
         nc.gpsimd.memset(v_tab_scales[:, : T // 8], 0)
         nc.vector.memset(v_tab_scales[:, T // 8 :], 0)
-        nc.gpsimd.memset(q_tab_scales[:], 0)
-        nc.gpsimd.memset(v_scales[:], 0)
-        d_scale_rows = keep.tile([P, PASSES, N // 4], I32, name="d_scale_rows", align_bytes=ALIGN)
-        nc.gpsimd.memset(d_scale_rows[:], 0)
+        nc.vector.memset(q_tab_scales[:], 0)
+        for rows in planes:
+            nc.vector.memset(rows[:], 0)
+        nc.vector.memset(d_scale_rows[:], 0)
 
         v_tab_words = keep.tile([P, T], I32, name="v_tab_words", tag="v_tab_words")
-        q_tab_words = keep.tile([P, T2], I32, name="q_tab_words", tag="w_raw1", align_bytes=ALIGN)
-        v_words_hbm = tab_words[0].rearrange("p t i -> p (t i)").bitcast(I32)
+        q_tab_words = keep.tile([P, T2], I32, name="q_tab_words")
         nc.sync.dma_start(v_list[:], offs)
-        nc.sync.dma_start(wg_sb[:], wg.rearrange("(g p t) -> p g t", p=P, t=SLOTS))
-        nc.sync.dma_start(v_tab_words[:, :V_FIRST], v_words_hbm[:, :V_FIRST])
-        nc.sync.dma_start(v_tab_scales[0:P:8], tab_scales[0].bitcast(I32))
         nc.sync.dma_start(q_list[:], offs2)
-        load_scale_rows(q_tab_scales, Q_ROW, tab2_scales[0], range(2))
-        nc.sync.dma_start(v_tab_words[:, V_FIRST:], v_words_hbm[:, V_FIRST:])
-        load_scale_rows(q_tab_scales, Q_ROW, tab2_scales[0], range(2, 4))
+        nc.sync.dma_start(wg_sb[:], wg.rearrange("(g p t) -> p g t", p=P, t=SLOTS))
+        nc.sync.dma_start(v_tab_scales[0:P:8], tab_scales[0].bitcast(I32))
+        nc.sync.dma_start(q_tab_scales[0:P:8], tab2_scales[0].bitcast(I32))
+        nc.sync.dma_start(v_tab_words[:], tab_words[0].rearrange("p t i -> p (t i)").bitcast(I32))
         nc.sync.dma_start(q_tab_words[:], tab2_words[0].rearrange("p t i -> p (t i)").bitcast(I32))
-        d_codes = keep.tile([P, PASSES, 2 * N // 4], I32, name="d_codes", align_bytes=ALIGN)
-        nc.sync.dma_start(d_codes[:], d_words.rearrange("g p b -> p g b").bitcast(I32))
-        load_scale_rows(d_scale_rows, 0, d_scales.rearrange("g r n -> r g n"))
 
         nc.scalar.activation(ln_wg[:], wg_sb[:].rearrange("p g t -> p (g t)"), ACT.Ln)
         for k in range(len(gate_tags)):
             nc.scalar.copy(ln_first[k][:], ln_wg[:, k % SLOTS : k % SLOTS + 1])
-        nc.scalar.copy(ln_late[:], ln_wg[:, SLOTS : 2 * SLOTS])
         nc.scalar.activation(warm[:], ln_wg[:, 0:1], ACT.Exp)
 
         q_words, v_words, v_scales_listed, w_raw, e_bf, den, num = {}, {}, {}, {}, {}, {}, {}
@@ -128,20 +124,27 @@ def tile_list_replay_kernel_control_kernel(
                 cols = slice(c * LIST_COLS + j.start // 16, c * LIST_COLS + j.stop // 16)
                 nc.vector.tensor_copy(q_words[c][:, j], q_tab_words[:].bitcast(U32).indirect(q_list[:, cols]))
 
-        def v_scale_plane():
-            listed = keep.tile([P, S], U8, name="v_scales_listed", align_bytes=ALIGN)
-            ordered = keep.tile([P, S], U8, name="v_scales_ordered", tag="w_raw0", align_bytes=ALIGN)
-            for g in range(PASSES):
-                i = slice(g * PASS, (g + 1) * PASS)
-                nc.vector.tensor_copy(listed[:, i], v_tab_scales[:].bitcast(U8).indirect(v_list[:, entries(g)]))
-            for g in range(PASSES):
-                i = slice(g * PASS, (g + 1) * PASS)
-                nc.vector.tensor_copy(
-                    ordered[:, i].rearrange("p (t m) -> p t m", t=SLOTS),
-                    listed[:, i].rearrange("p (m t) -> p t m", t=SLOTS),
-                )
+        listed = keep.tile([P, S], U8, name="v_scales_listed", align_bytes=ALIGN)
+        staged = [keep.tile([P, 2 * PASS], U8, name="staged%d" % k, align_bytes=ALIGN) for k in range(2)]
+        v_at = (0, 2 * PASS, 3 * PASS)
+        q_at = (PASS, 4 * PASS)
+
+        def gather_v_scales(g):
+            i = slice(g * PASS, (g + 1) * PASS)
+            nc.vector.tensor_copy(listed[:, i], v_tab_scales[:].bitcast(U8).indirect(v_list[:, entries(g)]))
+
+        def order_v_scales(g):
+            nc.vector.tensor_copy(
+                staged[v_at[g] // (2 * PASS)][:, v_at[g] % (2 * PASS) : v_at[g] % (2 * PASS) + PASS].rearrange("p (t m) -> p t m", t=SLOTS),
+                listed[:, g * PASS : (g + 1) * PASS].rearrange("p (m t) -> p t m", t=SLOTS),
+            )
+
+        def move_rows(first, rows):
             for r in range(4):
-                nc.scalar.dma_start(v_scales[V_ROW + r : P : 32], ordered[8 * r : P : 32].bitcast(I32))
+                nc.sync.dma_start(planes[first][V_ROW + r : P : 32], rows[8 * r : P : 32].bitcast(I32))
+
+        def plane(at, cols):
+            return planes[at // (2 * PASS)][V_ROW:P].bitcast(U8)[:, at % (2 * PASS) + cols.start : at % (2 * PASS) + cols.stop]
 
         def gather_v_words(g):
             v_words[g] = keep.tile([P, PASS], U32, name="v_words%d" % g, tag="v_words%d" % g, align_bytes=ALIGN)
@@ -183,18 +186,16 @@ def tile_list_replay_kernel_control_kernel(
                 nc.tensor.matmul_mx(
                     out=acc[:, j],
                     lhsT=v_words[g][:, m].bitcast(FP8X4),
-                    lhsT_scale=v_scales[V_ROW:P].bitcast(U8)[:, g * PASS + t * P : g * PASS + (t + 1) * P],
+                    lhsT_scale=plane(v_at[g], m),
                     rhs=q_words[c][:, j].bitcast(FP8X4),
-                    rhs_scale=q_scales[c][Q_ROW:P, j],
+                    rhs_scale=plane(q_at[c], j),
                     start=True,
                     stop=True,
                 )
                 col = g * SLOTS + t
                 bias = ln_wg[:, col : col + 1]
-                if (g, c) == (0, 0) and first_bank + t < len(ln_first):
-                    bias = ln_first[first_bank + t][:]
-                if (g, c) == (1, 1):
-                    bias = ln_late[:, t : t + 1]
+                if (g, c, j.start) == (0, 0, 0):
+                    bias = ln_first[t][:]
                 nc.scalar.activation(e_rows[g, c][:, t, j], acc[:, j], ACT.Exp, bias=bias)
 
         def interleave_e(g, c, parts=1):
@@ -212,22 +213,34 @@ def tile_list_replay_kernel_control_kernel(
                     in_=e_bf[g, c][:, j, :].rearrange("p j t -> p (j t)"),
                 )
 
-        v_scale_plane()
-        load_w(0)
+        gather_v_scales(0)
         gather_q_scales(0)
+        order_v_scales(0)
+        nc.vector.tensor_copy(staged[0][:, PASS:].bitcast(U32), q_scales[0][:].bitcast(U32))
+        move_rows(0, staged[0][:])
+        load_w(0)
+        gather_v_scales(1)
+        gather_v_scales(2)
+        order_v_scales(1)
+        order_v_scales(2)
+        move_rows(1, staged[1][:])
+        d_codes = keep.tile([P, PASSES, 2 * N // 4], I32, name="d_codes", align_bytes=ALIGN)
+        nc.sync.dma_start(d_codes[:], d_words.rearrange("g p b -> p g b").bitcast(I32))
+        load_scale_rows(d_scale_rows, 0, d_scales.rearrange("g r n -> r g n"))
+        load_w(1)
         gather_v_words(0)
         gather_q_words(0)
         gather_q_words(1)
-        load_w(1)
         kernel_values(0, 0, 0, slice(0, CHUNK // 2))
         kernel_values(0, 0, 4, slice(CHUNK // 2, CHUNK))
         gather_v_words(1)
-        gather_v_words(2)
         gather_q_scales(1)
+        move_rows(2, q_scales[1][:])
         load_w(2)
+        gather_v_words(2)
         kernel_values(1, 0, 0)
         kernel_values(2, 0, 4)
-        bn_sb = keep.tile([P, N_TILES], F32, name="bn_sb", tag="v_tab_words")
+        bn_sb = keep.tile([P, N_TILES], F32, name="bn_sb")
         with nc.allow_non_contiguous_dma(reason="one bias value a partition and row tile"):
             nc.sync.dma_start(bn_sb[:], bn.rearrange("(n p) -> p n", p=P))
         kernel_values(0, 1, 0)
@@ -269,20 +282,18 @@ def tile_list_replay_kernel_control_kernel(
         round_w_on_gpsimd(0)
         interleave_e(0, 0, 2)
         quantize_e(0, 0, 2)
-        den_passes(0, range(N_TILES), [0])
         interleave_e(1, 0)
         quantize_w(0)
         quantize_e(1, 0)
-        den_passes(0, range(N_TILES), [1])
         kernel_values(1, 1, 4)
+        kernel_values(2, 1, 0)
         interleave_e(2, 0, 2)
         quantize_e(2, 0, 2)
-        den_passes(0, range(N_TILES), [2])
+        den_passes(0, range(N_TILES), [0, 1, 2])
         den_squares = keep.tile([P, N_TILES, CHUNK], F32, name="den_squares", tag="den_squares")
         for n in range(N_TILES):
             scratch[n, 0] = den_squares[:, n, :]
             square_den(n, 0)
-        kernel_values(2, 1, 4)
         w_bf_late = keep.tile([P, 2, N, SLOTS], BF16, name="w_bf_late", tag="e_rows20", align_bytes=ALIGN)
         w_bf[1], w_bf[2] = w_bf_late[:, 0], w_bf_late[:, 1]
         num_passes(0, range(N_TILES), [0])
@@ -302,7 +313,7 @@ def tile_list_replay_kernel_control_kernel(
         quantize_e(2, 1, 2)
         den_passes(1, range(N_TILES), [2])
 
-        recip = keep.tile([P, N_TILES * CHUNKS, CHUNK], F32, name="recip", tag="recip")
+        recip = keep.tile([P, N_TILES * CHUNKS, CHUNK], F32, name="recip")
 
         ratios, cut = {}, {}
 

@@ -27,17 +27,22 @@ LIST_COLS = PASS // 16
 RUN = 4
 ALIGN = 64
 
-V_FIRST = 3 * T // 16
-V_ROW = 8
-Q_ROW = 4
-
-BANKS = 8
-NARROW_FROM = 16
-NUM_BANKS = ((0, 1, 2, 3), (0, 1, 2, 3))
-DEN_BANKS = ((4, 5, 6, 7), (4, 5, 6, 7))
-
-TWICE = 1
-HALVED = 3
+TAB_ROW = P - 16
+Q_FIRST = 3 * T2 // 4
+UNITS = [(g, c) for c in range(CHUNKS) for g in range(PASSES)]
+GATES = {
+    (0, 0, 0): "v_words1",
+    (0, 0, 1): "q_scales1",
+    (0, 0, 2): "v_words2",
+    (0, 1, 2): "w_raw1",
+    (0, 1, 3): "w_raw2",
+    (2, 0, 1): "e_words00",
+    (2, 0, 3): "e_words10",
+    (3, 0, 0): "w_words0",
+    (3, 0, 2): "e_words20",
+    (3, 0, 3): "w_bf_late",
+}
+TWICE = ((0, 0),)
 
 
 def tile_list_replay_kernel_control_kernel(
@@ -52,57 +57,51 @@ def tile_list_replay_kernel_control_kernel(
         def bank(b):
             return psum.tile([P, CHUNK], F32, name="bank%d" % b, tag="bank%d" % b)
 
-        def load_scale_rows(dst, first_row, rows, which=range(4)):
-            for r in which:
-                nc.sync.dma_start(dst[first_row + r : P : 32], rows[r:16:4].bitcast(I32))
-
         v_list = keep.tile([P, S // 16], U16, name="v_list")
         q_list = keep.tile([P, S2 // 16], U16, name="q_list")
         v_tab_scales = keep.tile([P, T // 4], I32, name="v_tab_scales", align_bytes=ALIGN)
         q_tab_scales = keep.tile([P, T2 // 4], I32, name="q_tab_scales", align_bytes=ALIGN)
         planes = [
-            keep.tile([P, cols // 4], I32, name="planes%d" % k, align_bytes=ALIGN)
-            for k, cols in enumerate((2 * PASS, 2 * PASS, CHUNK))
+            keep.tile([P, cols * PASS // 4], I32, name="planes%d" % k, align_bytes=ALIGN)
+            for k, cols in enumerate((2, 2, 1, 3))
         ]
-        d_scale_rows = keep.tile([P, PASSES, N // 4], I32, name="d_scale_rows", align_bytes=ALIGN)
         wg_sb = keep.tile([P, PASSES, SLOTS], F32, name="wg_sb")
         ln_wg = keep.tile([P, PASSES * SLOTS], F32, name="ln_wg", tag="den_squares")
-        gate_tags = ("v_words1", "q_scales1", "v_words2", "w_raw2")
-        ln_first = [
-            keep.tile([P, 1], F32, name="ln_first%d" % k, tag=tag, align_bytes=ALIGN) for k, tag in enumerate(gate_tags)
-        ]
+        gate_bias = {
+            key: keep.tile([P, 1], F32, name="bias_" + tag, tag=tag, align_bytes=ALIGN) for key, tag in GATES.items()
+        }
         warm = keep.tile([P, 1], F32, name="warm")
 
-        nc.gpsimd.memset(v_tab_scales[:, : T // 8], 0)
-        nc.vector.memset(v_tab_scales[:, T // 8 :], 0)
-        nc.vector.memset(q_tab_scales[:], 0)
+        nc.vector.memset(q_tab_scales[0:TAB_ROW], 0)
+        nc.vector.memset(v_tab_scales[0:TAB_ROW], 0)
         for rows in planes:
-            nc.vector.memset(rows[:], 0)
-        nc.vector.memset(d_scale_rows[:], 0)
+            nc.gpsimd.memset(rows[:], 0)
 
-        v_tab_words = keep.tile([P, T], I32, name="v_tab_words", tag="v_tab_words")
+        v_tab_words = keep.tile([P, T], I32, name="v_tab_words")
         q_tab_words = keep.tile([P, T2], I32, name="q_tab_words")
-        nc.sync.dma_start(v_list[:], offs)
+        q_tab_hbm = tab2_words[0].rearrange("p t i -> p (t i)").bitcast(I32)
+        nc.sync.dma_start(q_tab_scales[TAB_ROW:P], tab2_scales[0].bitcast(I32))
         nc.sync.dma_start(q_list[:], offs2)
-        nc.sync.dma_start(wg_sb[:], wg.rearrange("(g p t) -> p g t", p=P, t=SLOTS))
-        nc.sync.dma_start(v_tab_scales[0:P:8], tab_scales[0].bitcast(I32))
-        nc.sync.dma_start(q_tab_scales[0:P:8], tab2_scales[0].bitcast(I32))
+        nc.sync.dma_start(v_tab_scales[TAB_ROW:P], tab_scales[0].bitcast(I32))
+        nc.sync.dma_start(v_list[:], offs)
         nc.sync.dma_start(v_tab_words[:], tab_words[0].rearrange("p t i -> p (t i)").bitcast(I32))
-        nc.sync.dma_start(q_tab_words[:], tab2_words[0].rearrange("p t i -> p (t i)").bitcast(I32))
+        nc.sync.dma_start(wg_sb[:], wg.rearrange("(g p t) -> p g t", p=P, t=SLOTS))
+        staged = [keep.tile([P, 2 * PASS], U8, name="staged%d" % k, align_bytes=ALIGN) for k in range(2)]
+        nc.sync.dma_start(q_tab_words[:], q_tab_hbm)
 
         nc.scalar.activation(ln_wg[:], wg_sb[:].rearrange("p g t -> p (g t)"), ACT.Ln)
-        for k in range(len(gate_tags)):
-            nc.scalar.copy(ln_first[k][:], ln_wg[:, k % SLOTS : k % SLOTS + 1])
+        for (u, half, t), tile in gate_bias.items():
+            col = UNITS[u][0] * SLOTS + t
+            nc.scalar.copy(tile[:], ln_wg[:, col : col + 1])
         nc.scalar.activation(warm[:], ln_wg[:, 0:1], ACT.Exp)
 
-        q_words, v_words, v_scales_listed, w_raw, e_bf, den, num = {}, {}, {}, {}, {}, {}, {}
+        q_words, v_words, w_raw, e_bf, den, num = {}, {}, {}, {}, {}, {}
         q_scales = {}
-        units = [(g, c) for g in range(PASSES) for c in range(CHUNKS)]
-        e_words = {u: keep.tile([P, CHUNK], U32, name="e_words%d%d" % u, align_bytes=ALIGN) for u in units}
-        e_scales = {u: keep.tile([P, CHUNK], U8, name="e_scales%d%d" % u, align_bytes=ALIGN) for u in units}
+        e_words = {}
+        e_scales = {u: keep.tile([P, CHUNK], U8, name="e_scales%d%d" % u, align_bytes=ALIGN) for u in UNITS}
         e_rows = {
             u: keep.tile([P, SLOTS, CHUNK], BF16, name="e_rows%d%d" % u, tag="e_rows%d%d" % u, align_bytes=ALIGN)
-            for u in units
+            for u in UNITS
         }
         w_words, w_bf = {}, {}
         w_scales = [keep.tile([P, N], U8, name="w_scales%d" % g, align_bytes=ALIGN) for g in range(PASSES)]
@@ -125,26 +124,20 @@ def tile_list_replay_kernel_control_kernel(
                 nc.vector.tensor_copy(q_words[c][:, j], q_tab_words[:].bitcast(U32).indirect(q_list[:, cols]))
 
         listed = keep.tile([P, S], U8, name="v_scales_listed", align_bytes=ALIGN)
-        staged = [keep.tile([P, 2 * PASS], U8, name="staged%d" % k, align_bytes=ALIGN) for k in range(2)]
-        v_at = (0, 2 * PASS, 3 * PASS)
-        q_at = (PASS, 4 * PASS)
+        v_at = ((0, PASS), (1, 0), (1, PASS))
+        q_at = ((0, 0), (2, 0))
+        d_at = ((3, 0), (3, PASS), (3, 2 * PASS))
 
-        def gather_v_scales(g):
-            i = slice(g * PASS, (g + 1) * PASS)
-            nc.vector.tensor_copy(listed[:, i], v_tab_scales[:].bitcast(U8).indirect(v_list[:, entries(g)]))
+        def stage_q_scales(c):
+            nc.vector.tensor_copy(staged[0][:, :CHUNK].bitcast(U32), q_scales[c][:].bitcast(U32))
 
-        def order_v_scales(g):
-            nc.vector.tensor_copy(
-                staged[v_at[g] // (2 * PASS)][:, v_at[g] % (2 * PASS) : v_at[g] % (2 * PASS) + PASS].rearrange("p (t m) -> p t m", t=SLOTS),
-                listed[:, g * PASS : (g + 1) * PASS].rearrange("p (m t) -> p t m", t=SLOTS),
-            )
-
-        def move_rows(first, rows):
+        def move_rows(k, rows):
             for r in range(4):
-                nc.sync.dma_start(planes[first][V_ROW + r : P : 32], rows[8 * r : P : 32].bitcast(I32))
+                nc.sync.dma_start(planes[k][r:P:32], rows[TAB_ROW + r : P : 4].bitcast(I32))
 
-        def plane(at, cols):
-            return planes[at // (2 * PASS)][V_ROW:P].bitcast(U8)[:, at % (2 * PASS) + cols.start : at % (2 * PASS) + cols.stop]
+        def plane(place, cols):
+            k, at = place
+            return planes[k][:].bitcast(U8)[:, at + cols.start : at + cols.stop]
 
         def gather_v_words(g):
             v_words[g] = keep.tile([P, PASS], U32, name="v_words%d" % g, tag="v_words%d" % g, align_bytes=ALIGN)
@@ -153,33 +146,36 @@ def tile_list_replay_kernel_control_kernel(
                 v_tab_words[:].bitcast(U32).indirect(v_list[:, entries(g)]),
             )
 
-        def load_w(g):
-            w_raw[g] = keep.tile([P, SLOTS, N], F32, name="w_raw%d" % g, tag="w_raw%d" % g, align_bytes=ALIGN)
-            nc.sync.dma_start(w_raw[g][:], w[g * PASS : (g + 1) * PASS, :].rearrange("(p t) n -> p t n", t=SLOTS))
+        def load_w(g, ns=slice(0, N)):
+            key = (g, ns.start)
+            tag = "w_raw%d" % g if ns.start == 0 else "w_raw%d_%d" % key
+            w_raw[key] = keep.tile([P, SLOTS, ns.stop - ns.start], F32, name=tag, tag=tag, align_bytes=ALIGN)
+            nc.sync.dma_start(w_raw[key][:], w[g * PASS : (g + 1) * PASS, ns].rearrange("(p t) n -> p t n", t=SLOTS))
 
         def interleave(dst, src):
             nc.vector.tensor_copy(
                 dst.rearrange("p (c i) t -> p c t i", i=RUN), src.rearrange("p t (c i) -> p c t i", i=RUN)
             )
 
+        halves = [slice(0, N // 2), slice(N // 2, N)]
+
         def round_w_on_gpsimd(g):
-            for h in range(2):
-                ns = slice(h * N // 2, (h + 1) * N // 2)
+            for ns in halves:
                 nc.gpsimd.tensor_scalar(
-                    w_bf[g][:, ns, :], w_raw[g][:, :, ns].rearrange("p t n -> p n t"), 1.0, 0.0, ALU.mult, ALU.add
+                    w_bf[g][:, ns, :], w_raw[g, ns.start][:].rearrange("p t n -> p n t"), 1.0, 0.0, ALU.mult, ALU.add
                 )
 
         def round_w(g):
-            interleave(w_bf[g], w_raw[g][:])
+            interleave(w_bf[g], w_raw[g, 0][:])
 
         def quantize_w(g):
-            tag = "q_words0" if g == 0 else "w_words%d" % g
-            w_words[g] = keep.tile([P, N], U32, name="w_words%d" % g, tag=tag, align_bytes=ALIGN)
+            w_words[g] = keep.tile([P, N], U32, name="w_words%d" % g, tag="w_words%d" % g, align_bytes=ALIGN)
             nc.vector.quantize_mx(
                 out=w_words[g][:].bitcast(FP8X4), scales=w_scales[g][:], in_=w_bf[g].rearrange("p n t -> p (n t)")
             )
 
-        def kernel_values(g, c, first_bank, j=slice(0, CHUNK)):
+        def kernel_values(u, first_bank, half=0, j=slice(0, CHUNK)):
+            g, c = UNITS[u]
             for t in range(SLOTS):
                 acc = bank(first_bank + t)
                 m = slice(t * P, (t + 1) * P)
@@ -193,67 +189,82 @@ def tile_list_replay_kernel_control_kernel(
                     stop=True,
                 )
                 col = g * SLOTS + t
-                bias = ln_wg[:, col : col + 1]
-                if (g, c, j.start) == (0, 0, 0):
-                    bias = ln_first[t][:]
+                bias = gate_bias[u, half, t][:] if (u, half, t) in gate_bias else ln_wg[:, col : col + 1]
                 nc.scalar.activation(e_rows[g, c][:, t, j], acc[:, j], ACT.Exp, bias=bias)
 
-        def interleave_e(g, c, parts=1):
+        def interleave_e(g, c, parts=(slice(0, CHUNK),)):
             e_bf[g, c] = ring.tile([P, CHUNK, SLOTS], BF16, name="e_bf", align_bytes=ALIGN)
-            for j0 in range(0, CHUNK, CHUNK // parts):
-                j = slice(j0, j0 + CHUNK // parts)
+            for j in parts:
                 interleave(e_bf[g, c][:, j, :], e_rows[g, c][:, :, j])
 
-        def quantize_e(g, c, parts=1):
-            for j0 in range(0, CHUNK, CHUNK // parts):
-                j = slice(j0, j0 + CHUNK // parts)
+        def quantize_e(g, c, parts=(slice(0, CHUNK),)):
+            tag = "e_words%d%d" % (g, c)
+            e_words[g, c] = keep.tile([P, CHUNK], U32, name=tag, tag=tag, align_bytes=ALIGN)
+            for j in parts:
                 nc.vector.quantize_mx(
                     out=e_words[g, c][:, j].bitcast(FP8X4),
                     scales=e_scales[g, c][:, j],
                     in_=e_bf[g, c][:, j, :].rearrange("p j t -> p (j t)"),
                 )
 
-        gather_v_scales(0)
+        def gather_v_scales(g0, g1):
+            cols = slice(g0 * LIST_COLS, g1 * LIST_COLS)
+            nc.vector.tensor_copy(
+                listed[:, g0 * PASS : g1 * PASS], v_tab_scales[:].bitcast(U8).indirect(v_list[:, cols])
+            )
+
+        def order_v_scales(g0, g1, dst):
+            nc.vector.tensor_copy(
+                dst.rearrange("p (g t m) -> p t g m", t=SLOTS, m=P),
+                listed[:, g0 * PASS : g1 * PASS].rearrange("p (g m t) -> p t g m", t=SLOTS, m=P),
+            )
+
         gather_q_scales(0)
-        order_v_scales(0)
-        nc.vector.tensor_copy(staged[0][:, PASS:].bitcast(U32), q_scales[0][:].bitcast(U32))
+        gather_v_scales(0, 1)
+        stage_q_scales(0)
+        order_v_scales(0, 1, staged[0][:, PASS:])
         move_rows(0, staged[0][:])
-        load_w(0)
-        gather_v_scales(1)
-        gather_v_scales(2)
-        order_v_scales(1)
-        order_v_scales(2)
+        gather_v_scales(1, 3)
+        order_v_scales(1, 3, staged[1][:])
         move_rows(1, staged[1][:])
+        load_w(0, halves[0])
+        load_w(0, halves[1])
+        for r in range(4):
+            nc.sync.dma_start(
+                planes[3][r:P:32].rearrange("q (g n) -> q g n", g=PASSES),
+                d_scales.rearrange("g r n -> r g n")[r:16:4].bitcast(I32),
+            )
         d_codes = keep.tile([P, PASSES, 2 * N // 4], I32, name="d_codes", align_bytes=ALIGN)
         nc.sync.dma_start(d_codes[:], d_words.rearrange("g p b -> p g b").bitcast(I32))
-        load_scale_rows(d_scale_rows, 0, d_scales.rearrange("g r n -> r g n"))
-        load_w(1)
         gather_v_words(0)
         gather_q_words(0)
         gather_q_words(1)
-        kernel_values(0, 0, 0, slice(0, CHUNK // 2))
-        kernel_values(0, 0, 4, slice(CHUNK // 2, CHUNK))
+        kernel_values(0, 0, 0, halves[0])
+        kernel_values(0, 4, 1, halves[1])
         gather_v_words(1)
         gather_q_scales(1)
         move_rows(2, q_scales[1][:])
+        load_w(1)
         load_w(2)
         gather_v_words(2)
-        kernel_values(1, 0, 0)
-        kernel_values(2, 0, 4)
+        kernel_values(1, 0)
+        kernel_values(2, 4)
         bn_sb = keep.tile([P, N_TILES], F32, name="bn_sb")
         with nc.allow_non_contiguous_dma(reason="one bias value a partition and row tile"):
             nc.sync.dma_start(bn_sb[:], bn.rearrange("(n p) -> p n", p=P))
-        kernel_values(0, 1, 0)
+        kernel_values(3, 0)
+        kernel_values(4, 4)
+        kernel_values(5, 4)
 
         def den_passes(c, tiles, passes):
-            for n in tiles:
-                if passes[0] == 0:
-                    den[n, c] = bank(DEN_BANKS[c][n])
-                for g in passes:
+            for g in passes:
+                for n in tiles:
+                    if g == 0:
+                        den[n, c] = bank(n)
                     nc.tensor.matmul_mx(
                         out=den[n, c][:],
                         lhsT=d_codes[:, g, n * 2 * P // 4 : (n + 1) * 2 * P // 4].bitcast(U8).bitcast(FP4X4),
-                        lhsT_scale=d_scale_rows[:, g, n * P // 4 : (n + 1) * P // 4].bitcast(U8),
+                        lhsT_scale=plane(d_at[g], slice(n * P, (n + 1) * P)),
                         rhs=e_words[g, c][:].bitcast(FP8X4),
                         rhs_scale=e_scales[g, c][:],
                         start=(g == 0),
@@ -261,11 +272,11 @@ def tile_list_replay_kernel_control_kernel(
                     )
 
         def num_passes(c, tiles, passes):
-            for n in tiles:
-                if passes[0] == 0:
-                    num[n, c] = bank(NUM_BANKS[c][n])
-                m = slice(n * P, (n + 1) * P)
-                for g in passes:
+            for g in passes:
+                for n in tiles:
+                    if g == 0:
+                        num[n, c] = bank(N_TILES + n)
+                    m = slice(n * P, (n + 1) * P)
                     nc.tensor.matmul_mx(
                         out=num[n, c][:],
                         lhsT=w_words[g][:, m].bitcast(FP8X4),
@@ -280,58 +291,54 @@ def tile_list_replay_kernel_control_kernel(
             nc.scalar.activation(scratch[n, c], den[n, c][:], ACT.Square)
 
         round_w_on_gpsimd(0)
-        interleave_e(0, 0, 2)
-        quantize_e(0, 0, 2)
+        interleave_e(0, 0)
         interleave_e(1, 0)
-        quantize_w(0)
+        quantize_e(0, 0)
         quantize_e(1, 0)
-        kernel_values(1, 1, 4)
-        kernel_values(2, 1, 0)
-        interleave_e(2, 0, 2)
-        quantize_e(2, 0, 2)
+        interleave_e(2, 0)
+        quantize_w(0)
+        quantize_e(2, 0)
         den_passes(0, range(N_TILES), [0, 1, 2])
         den_squares = keep.tile([P, N_TILES, CHUNK], F32, name="den_squares", tag="den_squares")
         for n in range(N_TILES):
             scratch[n, 0] = den_squares[:, n, :]
-            square_den(n, 0)
-        w_bf_late = keep.tile([P, 2, N, SLOTS], BF16, name="w_bf_late", tag="e_rows20", align_bytes=ALIGN)
+            if (n, 0) not in TWICE:
+                square_den(n, 0)
+        w_bf_late = keep.tile([P, 2, N, SLOTS], BF16, name="w_bf_late", tag="w_bf_late", align_bytes=ALIGN)
         w_bf[1], w_bf[2] = w_bf_late[:, 0], w_bf_late[:, 1]
-        num_passes(0, range(N_TILES), [0])
         round_w(1)
         round_w(2)
         quantize_w(1)
-        num_passes(0, range(N_TILES), [1])
-        interleave_e(0, 1)
         quantize_w(2)
-        num_passes(0, range(N_TILES), [2])
+        num_passes(0, range(N_TILES), [0, 1, 2])
+        interleave_e(0, 1)
         interleave_e(1, 1)
         quantize_e(0, 1)
-        den_passes(1, range(N_TILES), [0])
         quantize_e(1, 1)
-        den_passes(1, range(N_TILES), [1])
-        interleave_e(2, 1, 2)
-        quantize_e(2, 1, 2)
-        den_passes(1, range(N_TILES), [2])
+        interleave_e(2, 1, halves)
+        quantize_e(2, 1, halves)
+        den_passes(1, [n for n in range(N_TILES) if (n, 0) not in TWICE], [0, 1])
 
         recip = keep.tile([P, N_TILES * CHUNKS, CHUNK], F32, name="recip")
-
         ratios, cut = {}, {}
 
-        def inverse(n, c, twice, halved):
-            cuts = (0, CHUNK // 2, 3 * CHUNK // 4, CHUNK) if halved else (0, CHUNK)
+        def inverse(n, c, fine=False):
+            cuts = (0, CHUNK // 2, 3 * CHUNK // 4, CHUNK) if fine else (0, CHUNK)
             cut[n, c] = [slice(j0, j1) for j0, j1 in zip(cuts, cuts[1:])]
-            radicand = den[n, c] if twice else scratch[n, c]
             for j in cut[n, c]:
-                nc.scalar.activation(recip[:, c * N_TILES + n, j], radicand[:, j], ACT.Abs_reciprocal_sqrt)
+                if (n, c) in TWICE:
+                    nc.scalar.activation(scratch[n, c][:, j], den[n, c][:, j], ACT.Abs_reciprocal_sqrt)
+                else:
+                    nc.scalar.activation(recip[:, c * N_TILES + n, j], scratch[n, c][:, j], ACT.Abs_reciprocal_sqrt)
 
-        def divide(n, c, twice):
-            r = recip[:, c * N_TILES + n, :]
+        def divide(n, c):
+            r = scratch[n, c] if (n, c) in TWICE else recip[:, c * N_TILES + n, :]
             ratio = keep.tile([P, CHUNK], F32, name="ratio%d%d" % (n, c))
             for j in cut[n, c]:
                 nc.vector.tensor_tensor(ratio[:, j], num[n, c][:, j], r[:, j], ALU.mult)
-            if twice:
-                nc.vector.tensor_tensor(scratch[n, c], ratio[:], r, ALU.mult)
-                ratio = scratch[n, c]
+            if (n, c) in TWICE:
+                nc.vector.tensor_tensor(recip[:, c * N_TILES + n, :], ratio[:], r, ALU.mult)
+                ratio = recip[:, c * N_TILES + n, :]
             ratios[n, c] = ratio
 
         def add_bias_and_store(n, c, engine):
@@ -345,23 +352,29 @@ def tile_list_replay_kernel_control_kernel(
                     adder.tensor_scalar(res[:, j], ratios[n, c][:, j], 1.0, bias, ALU.mult, ALU.add)
                 nc.sync.dma_start(out[n * P : (n + 1) * P, c * CHUNK + j.start : c * CHUNK + j.stop], res[:, j])
 
-        def finish(n, c, twice):
-            inverse(n, c, twice, False)
-            divide(n, c, twice)
+        def finish(n, c):
+            inverse(n, c)
+            divide(n, c)
             add_bias_and_store(n, c, "gpsimd")
 
         for n in range(N_TILES):
-            finish(n, 0, False)
+            inverse(n, 0)
+        den_passes(1, [n for n in range(N_TILES) if (n, 0) in TWICE], [0, 1])
+        den_passes(1, range(N_TILES), [2])
+        for n in range(N_TILES):
+            divide(n, 0)
+            add_bias_and_store(n, 0, "gpsimd")
             num_passes(1, [n], [0, 1, 2])
-        square_den(0, 1)
-        square_den(1, 1)
-        finish(0, 1, False)
-        finish(1, 1, False)
+        for n in (0, 1):
+            if (n, 1) not in TWICE:
+                square_den(n, 1)
+        finish(0, 1)
+        finish(1, 1)
         square_den(2, 1)
         square_den(3, 1)
-        inverse(2, 1, False, False)
-        divide(2, 1, False)
-        inverse(3, 1, False, True)
+        inverse(2, 1)
+        divide(2, 1)
+        inverse(3, 1, True)
         add_bias_and_store(2, 1, "scalar")
-        divide(3, 1, False)
+        divide(3, 1)
         add_bias_and_store(3, 1, "vector")

@@ -28,21 +28,26 @@ RUN = 4
 ALIGN = 64
 
 TAB_ROW = P - 16
-Q_FIRST = 3 * T2 // 4
-UNITS = [(g, c) for c in range(CHUNKS) for g in range(PASSES)]
-GATES = {
-    (0, 0, 0): "v_words1",
-    (0, 0, 1): "q_scales1",
-    (0, 0, 2): "v_words2",
-    (0, 1, 2): "w_raw1",
-    (0, 1, 3): "w_raw2",
-    (2, 0, 1): "e_words00",
-    (2, 0, 3): "e_words10",
-    (3, 0, 0): "w_words0",
-    (3, 0, 2): "e_words20",
-    (3, 0, 3): "w_bf_late",
+UNITS = [(0, 0), (0, 1), (1, 0), (2, 0), (1, 1), (2, 1)]
+HELD = {
+    (0, 0, 0): "listed2",
+    (0, 0, 1): "plane_d",
+    (0, 0, 2): "w_bf0",
+    (0, 0, 3): "v_words1",
+    (0, 1, 0): "d_codes",
+    (0, 1, 2): "staged2",
+    (1, 0, 0): "v_words2",
+    (1, 0, 2): "e_bf00",
+    (2, 0, 3): "w_words0",
+    (3, 0, 0): "bn_sb",
+    (3, 0, 3): "w_words1",
+    (4, 0, 2): "e_words20",
+    (4, 0, 3): "e_words01",
+    (5, 0, 0): "e_bf11",
+    (5, 0, 1): "w_bf2",
 }
 TWICE = ((0, 0),)
+ODD = 63
 
 
 def tile_list_replay_kernel_control_kernel(
@@ -51,125 +56,102 @@ def tile_list_replay_kernel_control_kernel(
     nc = tc.nc
     with ExitStack() as ctx:
         keep = ctx.enter_context(tc.tile_pool(name="keep", bufs=1))
-        ring = ctx.enter_context(tc.tile_pool(name="ring", bufs=3))
         psum = ctx.enter_context(tc.psum_pool(name="psum", bufs=1))
 
         def bank(b):
             return psum.tile([P, CHUNK], F32, name="bank%d" % b, tag="bank%d" % b)
 
+        def tagged(tag, shape, dtype, name=None):
+            return keep.tile(shape, dtype, name=name or tag, tag=tag, align_bytes=ALIGN)
+
         v_list = keep.tile([P, S // 16], U16, name="v_list")
         q_list = keep.tile([P, S2 // 16], U16, name="q_list")
-        v_tab_scales = keep.tile([P, T // 4], I32, name="v_tab_scales", align_bytes=ALIGN)
-        q_tab_scales = keep.tile([P, T2 // 4], I32, name="q_tab_scales", align_bytes=ALIGN)
-        planes = [
-            keep.tile([P, cols * PASS // 4], I32, name="planes%d" % k, align_bytes=ALIGN)
-            for k, cols in enumerate((2, 2, 1, 3))
-        ]
-        wg_sb = keep.tile([P, PASSES, SLOTS], F32, name="wg_sb")
-        ln_wg = keep.tile([P, PASSES * SLOTS], F32, name="ln_wg", tag="den_squares")
-        gate_bias = {
-            key: keep.tile([P, 1], F32, name="bias_" + tag, tag=tag, align_bytes=ALIGN) for key, tag in GATES.items()
-        }
-        warm = keep.tile([P, 1], F32, name="warm")
-
-        nc.vector.memset(q_tab_scales[0:TAB_ROW], 0)
-        nc.vector.memset(v_tab_scales[0:TAB_ROW], 0)
-        for rows in planes:
-            nc.gpsimd.memset(rows[:], 0)
-
+        v_tab_scales = tagged("v_tab_scales", [P, T // 4], I32)
+        q_tab_scales = tagged("q_tab_scales", [P, T2 // 4], I32)
         v_tab_words = keep.tile([P, T], I32, name="v_tab_words")
         q_tab_words = keep.tile([P, T2], I32, name="q_tab_words")
-        q_tab_hbm = tab2_words[0].rearrange("p t i -> p (t i)").bitcast(I32)
-        nc.sync.dma_start(q_tab_scales[TAB_ROW:P], tab2_scales[0].bitcast(I32))
-        nc.sync.dma_start(q_list[:], offs2)
-        nc.sync.dma_start(v_tab_scales[TAB_ROW:P], tab_scales[0].bitcast(I32))
+        wg_sb = keep.tile([P, PASSES, SLOTS], F32, name="wg_sb")
+        ln_wg = keep.tile([P, PASSES * SLOTS], F32, name="ln_wg", tag="den_squares")
+        held_bias = {key: tagged(tag, [P, 1], F32, "bias_" + tag) for key, tag in HELD.items()}
+        warm = keep.tile([P, 1], F32, name="warm")
+
+        nc.vector.memset(v_tab_scales[0:TAB_ROW], 0)
+        nc.vector.memset(q_tab_scales[0:TAB_ROW], 0)
+        plane_first = tagged("plane_first", [P, (2 * PASS + S2) // 4], I32)
+        plane_v2 = tagged("plane_v2", [P, PASS // 4], I32)
+        nc.gpsimd.memset(plane_first[:], 0)
+        nc.gpsimd.memset(plane_v2[:], 0)
+
         nc.sync.dma_start(v_list[:], offs)
+        nc.scalar.dma_start(v_tab_scales[TAB_ROW:P], tab_scales[0].bitcast(I32))
+        nc.sync.dma_start(q_list[:], offs2)
+        nc.scalar.dma_start(q_tab_scales[TAB_ROW:P], tab2_scales[0].bitcast(I32))
         nc.sync.dma_start(v_tab_words[:], tab_words[0].rearrange("p t i -> p (t i)").bitcast(I32))
-        nc.sync.dma_start(wg_sb[:], wg.rearrange("(g p t) -> p g t", p=P, t=SLOTS))
-        staged = [keep.tile([P, 2 * PASS], U8, name="staged%d" % k, align_bytes=ALIGN) for k in range(2)]
-        nc.sync.dma_start(q_tab_words[:], q_tab_hbm)
+        nc.scalar.dma_start(wg_sb[:], wg.rearrange("(g p t) -> p g t", p=P, t=SLOTS))
+        nc.sync.dma_start(q_tab_words[:], tab2_words[0].rearrange("p t i -> p (t i)").bitcast(I32))
 
         nc.scalar.activation(ln_wg[:], wg_sb[:].rearrange("p g t -> p (g t)"), ACT.Ln)
-        for (u, half, t), tile in gate_bias.items():
+        for (u, half, t), tile in held_bias.items():
             col = UNITS[u][0] * SLOTS + t
             nc.scalar.copy(tile[:], ln_wg[:, col : col + 1])
         nc.scalar.activation(warm[:], ln_wg[:, 0:1], ACT.Exp)
 
         q_words, v_words, w_raw, e_bf, den, num = {}, {}, {}, {}, {}, {}
-        q_scales = {}
-        e_words = {}
-        e_scales = {u: keep.tile([P, CHUNK], U8, name="e_scales%d%d" % u, align_bytes=ALIGN) for u in UNITS}
-        e_rows = {
-            u: keep.tile([P, SLOTS, CHUNK], BF16, name="e_rows%d%d" % u, tag="e_rows%d%d" % u, align_bytes=ALIGN)
-            for u in UNITS
-        }
-        w_words, w_bf = {}, {}
-        w_scales = [keep.tile([P, N], U8, name="w_scales%d" % g, align_bytes=ALIGN) for g in range(PASSES)]
-        w_bf[0] = keep.tile([P, N, SLOTS], BF16, name="w_bf0", align_bytes=ALIGN)[:]
+        e_words, w_words, w_bf, v_plane, q_plane = {}, {}, {}, {}, {}
+        e_scales = {u: tagged("e_scales%d%d" % u, [P, CHUNK], U8) for u in UNITS}
+        e_rows = {u: tagged("e_rows%d%d" % u, [P, SLOTS, CHUNK], BF16) for u in UNITS}
+        w_scales = [tagged("w_scales%d" % g, [P, N], U8) for g in range(PASSES)]
         scratch = {(n, 1): keep.tile([P, CHUNK], F32, name="scratch%d" % n)[:] for n in range(N_TILES)}
+        halves = [slice(0, CHUNK // 2), slice(CHUNK // 2, CHUNK)]
 
-        def entries(k):
-            return slice(k * LIST_COLS, (k + 1) * LIST_COLS)
+        def entries(k0, k1):
+            return slice(k0 // 16, k1 // 16)
 
-        def gather_q_scales(c):
-            q_scales[c] = keep.tile([P, CHUNK], U8, name="q_scales%d" % c, tag="q_scales%d" % c, align_bytes=ALIGN)
-            nc.vector.tensor_copy(q_scales[c][:], q_tab_scales[:].bitcast(U8).indirect(q_list[:, entries(c)]))
-
-        def gather_q_words(c):
-            q_words[c] = keep.tile([P, CHUNK], U32, name="q_words%d" % c, tag="q_words%d" % c, align_bytes=ALIGN)
-            parts = 2 if c == 0 else 1
-            for h in range(parts):
-                j = slice(h * CHUNK // parts, (h + 1) * CHUNK // parts)
-                cols = slice(c * LIST_COLS + j.start // 16, c * LIST_COLS + j.stop // 16)
+        def gather_q_words(c, parts):
+            q_words[c] = tagged("q_words%d" % c, [P, CHUNK], U32)
+            for j in parts:
+                cols = entries(c * CHUNK + j.start, c * CHUNK + j.stop)
                 nc.vector.tensor_copy(q_words[c][:, j], q_tab_words[:].bitcast(U32).indirect(q_list[:, cols]))
 
-        listed = keep.tile([P, S], U8, name="v_scales_listed", align_bytes=ALIGN)
-        v_at = ((0, PASS), (1, 0), (1, PASS))
-        q_at = ((0, 0), (2, 0))
-        d_at = ((3, 0), (3, PASS), (3, 2 * PASS))
-
-        def stage_q_scales(c):
-            nc.vector.tensor_copy(staged[0][:, :CHUNK].bitcast(U32), q_scales[c][:].bitcast(U32))
-
-        def move_rows(k, rows):
-            for r in range(4):
-                nc.sync.dma_start(planes[k][r:P:32], rows[TAB_ROW + r : P : 4].bitcast(I32))
-
-        def plane(place, cols):
-            k, at = place
-            return planes[k][:].bitcast(U8)[:, at + cols.start : at + cols.stop]
+        def gather_v_scales(g0, g1):
+            listed = tagged("listed%d" % g0, [P, (g1 - g0) * PASS], U8)
+            cols = entries(g0 * PASS, g1 * PASS)
+            nc.vector.tensor_copy(listed[:], v_tab_scales[:].bitcast(U8).indirect(v_list[:, cols]))
+            return listed
 
         def gather_v_words(g):
-            v_words[g] = keep.tile([P, PASS], U32, name="v_words%d" % g, tag="v_words%d" % g, align_bytes=ALIGN)
+            v_words[g] = tagged("v_words%d" % g, [P, PASS], U32)
             nc.vector.tensor_copy(
                 v_words[g][:].rearrange("p (t m) -> p m t", t=SLOTS),
-                v_tab_words[:].bitcast(U32).indirect(v_list[:, entries(g)]),
+                v_tab_words[:].bitcast(U32).indirect(v_list[:, entries(g * PASS, (g + 1) * PASS)]),
             )
 
-        def load_w(g, ns=slice(0, N)):
-            key = (g, ns.start)
-            tag = "w_raw%d" % g if ns.start == 0 else "w_raw%d_%d" % key
-            w_raw[key] = keep.tile([P, SLOTS, ns.stop - ns.start], F32, name=tag, tag=tag, align_bytes=ALIGN)
-            nc.sync.dma_start(w_raw[key][:], w[g * PASS : (g + 1) * PASS, ns].rearrange("(p t) n -> p t n", t=SLOTS))
+        def move_rows(queue, plane, rows):
+            for r in range(4):
+                queue.dma_start(plane[r:P:32], rows[TAB_ROW + r : P : 4].bitcast(I32))
+
+        def load_w(g, ns, dst):
+            w_raw[g, ns.start] = dst
+            nc.sync.dma_start(dst, w[g * PASS : (g + 1) * PASS, ns].rearrange("(p t) n -> p t n", t=SLOTS))
 
         def interleave(dst, src):
             nc.vector.tensor_copy(
                 dst.rearrange("p (c i) t -> p c t i", i=RUN), src.rearrange("p t (c i) -> p c t i", i=RUN)
             )
 
-        halves = [slice(0, N // 2), slice(N // 2, N)]
-
         def round_w_on_gpsimd(g):
+            w_bf[g] = tagged("w_bf%d" % g, [P, N, SLOTS], BF16)[:]
             for ns in halves:
                 nc.gpsimd.tensor_scalar(
-                    w_bf[g][:, ns, :], w_raw[g, ns.start][:].rearrange("p t n -> p n t"), 1.0, 0.0, ALU.mult, ALU.add
+                    w_bf[g][:, ns, :], w_raw[g, ns.start].rearrange("p t n -> p n t"), 1.0, 0.0, ALU.mult, ALU.add
                 )
 
         def round_w(g):
-            interleave(w_bf[g], w_raw[g, 0][:])
+            w_bf[g] = tagged("w_bf%d" % g, [P, N, SLOTS], BF16)[:]
+            interleave(w_bf[g], w_raw[g, 0])
 
         def quantize_w(g):
-            w_words[g] = keep.tile([P, N], U32, name="w_words%d" % g, tag="w_words%d" % g, align_bytes=ALIGN)
+            w_words[g] = tagged("w_words%d" % g, [P, N], U32)
             nc.vector.quantize_mx(
                 out=w_words[g][:].bitcast(FP8X4), scales=w_scales[g][:], in_=w_bf[g].rearrange("p n t -> p (n t)")
             )
@@ -182,77 +164,83 @@ def tile_list_replay_kernel_control_kernel(
                 nc.tensor.matmul_mx(
                     out=acc[:, j],
                     lhsT=v_words[g][:, m].bitcast(FP8X4),
-                    lhsT_scale=plane(v_at[g], m),
+                    lhsT_scale=v_plane[g][:, m],
                     rhs=q_words[c][:, j].bitcast(FP8X4),
-                    rhs_scale=plane(q_at[c], j),
+                    rhs_scale=q_plane[c][:, j],
                     start=True,
                     stop=True,
                 )
                 col = g * SLOTS + t
-                bias = gate_bias[u, half, t][:] if (u, half, t) in gate_bias else ln_wg[:, col : col + 1]
+                bias = held_bias[u, half, t][:] if (u, half, t) in held_bias else ln_wg[:, col : col + 1]
                 nc.scalar.activation(e_rows[g, c][:, t, j], acc[:, j], ACT.Exp, bias=bias)
 
-        def interleave_e(g, c, parts=(slice(0, CHUNK),)):
-            e_bf[g, c] = ring.tile([P, CHUNK, SLOTS], BF16, name="e_bf", align_bytes=ALIGN)
-            for j in parts:
-                interleave(e_bf[g, c][:, j, :], e_rows[g, c][:, :, j])
+        def interleave_e(g, c, j=slice(0, CHUNK)):
+            if j.start == 0:
+                e_bf[g, c] = tagged("e_bf%d%d" % (g, c), [P, CHUNK, SLOTS], BF16)
+            interleave(e_bf[g, c][:, j, :], e_rows[g, c][:, :, j])
 
-        def quantize_e(g, c, parts=(slice(0, CHUNK),)):
-            tag = "e_words%d%d" % (g, c)
-            e_words[g, c] = keep.tile([P, CHUNK], U32, name=tag, tag=tag, align_bytes=ALIGN)
-            for j in parts:
-                nc.vector.quantize_mx(
-                    out=e_words[g, c][:, j].bitcast(FP8X4),
-                    scales=e_scales[g, c][:, j],
-                    in_=e_bf[g, c][:, j, :].rearrange("p j t -> p (j t)"),
-                )
-
-        def gather_v_scales(g0, g1):
-            cols = slice(g0 * LIST_COLS, g1 * LIST_COLS)
-            nc.vector.tensor_copy(
-                listed[:, g0 * PASS : g1 * PASS], v_tab_scales[:].bitcast(U8).indirect(v_list[:, cols])
+        def quantize_e(g, c, j=slice(0, CHUNK)):
+            if j.start == 0:
+                e_words[g, c] = tagged("e_words%d%d" % (g, c), [P, CHUNK], U32)
+            nc.vector.quantize_mx(
+                out=e_words[g, c][:, j].bitcast(FP8X4),
+                scales=e_scales[g, c][:, j],
+                in_=e_bf[g, c][:, j, :].rearrange("p j t -> p (j t)"),
             )
 
-        def order_v_scales(g0, g1, dst):
-            nc.vector.tensor_copy(
-                dst.rearrange("p (g t m) -> p t g m", t=SLOTS, m=P),
-                listed[:, g0 * PASS : g1 * PASS].rearrange("p (g m t) -> p t g m", t=SLOTS, m=P),
-            )
-
-        gather_q_scales(0)
-        gather_v_scales(0, 1)
-        stage_q_scales(0)
-        order_v_scales(0, 1, staged[0][:, PASS:])
-        move_rows(0, staged[0][:])
-        gather_v_scales(1, 3)
-        order_v_scales(1, 3, staged[1][:])
-        move_rows(1, staged[1][:])
-        load_w(0, halves[0])
-        load_w(0, halves[1])
-        for r in range(4):
-            nc.sync.dma_start(
-                planes[3][r:P:32].rearrange("q (g n) -> q g n", g=PASSES),
-                d_scales.rearrange("g r n -> r g n")[r:16:4].bitcast(I32),
-            )
-        d_codes = keep.tile([P, PASSES, 2 * N // 4], I32, name="d_codes", align_bytes=ALIGN)
-        nc.sync.dma_start(d_codes[:], d_words.rearrange("g p b -> p g b").bitcast(I32))
+        listed = gather_v_scales(0, 2)
+        q_scales = tagged("q_scales", [P, S2], U8)
+        nc.vector.tensor_copy(q_scales[:], q_tab_scales[:].bitcast(U8).indirect(q_list[:]))
+        staged = tagged("staged", [P, 2 * PASS + S2], U8)
+        nc.vector.tensor_copy(
+            staged[:, : 2 * PASS].rearrange("p (g t m) -> p t g m", t=SLOTS, m=P),
+            listed[:].rearrange("p (g m t) -> p t g m", t=SLOTS, m=P),
+        )
+        nc.vector.tensor_copy(staged[:, 2 * PASS :].bitcast(U32), q_scales[:].bitcast(U32))
+        move_rows(nc.sync, plane_first, staged[:])
+        w_early = tagged("q_scales", [P, 3, SLOTS, N // 2], F32, "w_early")
+        load_w(0, halves[0], w_early[:, 0])
+        load_w(0, halves[1], w_early[:, 1])
+        load_w(1, halves[0], w_early[:, 2])
+        first_bytes = plane_first[:].bitcast(U8)
+        v_plane[0], v_plane[1] = first_bytes[:, :PASS], first_bytes[:, PASS : 2 * PASS]
+        q_plane[0], q_plane[1] = first_bytes[:, 2 * PASS : 2 * PASS + CHUNK], first_bytes[:, 2 * PASS + CHUNK :]
+        load_w(1, halves[1], tagged("staged", [P, SLOTS, N // 2], F32, "w_raw11")[:])
         gather_v_words(0)
-        gather_q_words(0)
-        gather_q_words(1)
+        gather_q_words(0, halves)
+        gather_q_words(1, [slice(0, CHUNK)])
         kernel_values(0, 0, 0, halves[0])
         kernel_values(0, 4, 1, halves[1])
+        listed2 = gather_v_scales(2, 3)
         gather_v_words(1)
-        gather_q_scales(1)
-        move_rows(2, q_scales[1][:])
-        load_w(1)
-        load_w(2)
+        plane_d = tagged("plane_d", [P, PASSES * N // 4], I32)
+        nc.gpsimd.memset(plane_d[:], 0)
+        for r in range(4):
+            nc.sync.dma_start(
+                plane_d[r:P:32].rearrange("q (g n) -> q g n", g=PASSES),
+                d_scales.rearrange("g r n -> r g n")[r:16:4].bitcast(I32),
+            )
+        d_plane = plane_d[:].bitcast(U8)
+        d_codes = tagged("d_codes", [P, PASSES, 2 * N // 4], I32)
+        nc.sync.dma_start(d_codes[:], d_words.rearrange("g p b -> p g b").bitcast(I32))
+        staged2 = tagged("staged2", [P, PASS], U8)
+        for m in (slice(0, ODD), slice(ODD, P)):
+            nc.vector.tensor_copy(
+                staged2[:].rearrange("p (t m) -> p m t", t=SLOTS)[:, m, :],
+                listed2[:].rearrange("p (m t) -> p m t", t=SLOTS)[:, m, :],
+            )
+        move_rows(nc.sync, plane_v2, staged2[:])
+        v_plane[2] = plane_v2[:].bitcast(U8)
+        load_w(2, slice(0, N), tagged("listed2", [P, SLOTS, N], F32, "w_raw2")[:])
         gather_v_words(2)
+        round_w_on_gpsimd(0)
+        round_w_on_gpsimd(1)
         kernel_values(1, 0)
         kernel_values(2, 4)
-        bn_sb = keep.tile([P, N_TILES], F32, name="bn_sb")
+        kernel_values(3, 0)
+        bn_sb = tagged("bn_sb", [P, N_TILES], F32)
         with nc.allow_non_contiguous_dma(reason="one bias value a partition and row tile"):
             nc.sync.dma_start(bn_sb[:], bn.rearrange("(n p) -> p n", p=P))
-        kernel_values(3, 0)
         kernel_values(4, 4)
         kernel_values(5, 4)
 
@@ -264,7 +252,7 @@ def tile_list_replay_kernel_control_kernel(
                     nc.tensor.matmul_mx(
                         out=den[n, c][:],
                         lhsT=d_codes[:, g, n * 2 * P // 4 : (n + 1) * 2 * P // 4].bitcast(U8).bitcast(FP4X4),
-                        lhsT_scale=plane(d_at[g], slice(n * P, (n + 1) * P)),
+                        lhsT_scale=d_plane[:, g * N + n * P : g * N + (n + 1) * P],
                         rhs=e_words[g, c][:].bitcast(FP8X4),
                         rhs_scale=e_scales[g, c][:],
                         start=(g == 0),
@@ -290,13 +278,14 @@ def tile_list_replay_kernel_control_kernel(
         def square_den(n, c):
             nc.scalar.activation(scratch[n, c], den[n, c][:], ACT.Square)
 
-        round_w_on_gpsimd(0)
         interleave_e(0, 0)
-        interleave_e(1, 0)
+        interleave_e(0, 1)
         quantize_e(0, 0)
+        interleave_e(1, 0)
+        quantize_w(0)
         quantize_e(1, 0)
         interleave_e(2, 0)
-        quantize_w(0)
+        quantize_w(1)
         quantize_e(2, 0)
         den_passes(0, range(N_TILES), [0, 1, 2])
         den_squares = keep.tile([P, N_TILES, CHUNK], F32, name="den_squares", tag="den_squares")
@@ -304,19 +293,16 @@ def tile_list_replay_kernel_control_kernel(
             scratch[n, 0] = den_squares[:, n, :]
             if (n, 0) not in TWICE:
                 square_den(n, 0)
-        w_bf_late = keep.tile([P, 2, N, SLOTS], BF16, name="w_bf_late", tag="w_bf_late", align_bytes=ALIGN)
-        w_bf[1], w_bf[2] = w_bf_late[:, 0], w_bf_late[:, 1]
-        round_w(1)
-        round_w(2)
-        quantize_w(1)
-        quantize_w(2)
-        num_passes(0, range(N_TILES), [0, 1, 2])
-        interleave_e(0, 1)
-        interleave_e(1, 1)
         quantize_e(0, 1)
+        interleave_e(1, 1)
+        round_w(2)
         quantize_e(1, 1)
-        interleave_e(2, 1, halves)
-        quantize_e(2, 1, halves)
+        interleave_e(2, 1, halves[0])
+        quantize_w(2)
+        interleave_e(2, 1, halves[1])
+        quantize_e(2, 1, halves[0])
+        quantize_e(2, 1, halves[1])
+        num_passes(0, range(N_TILES), [0, 1, 2])
         den_passes(1, [n for n in range(N_TILES) if (n, 0) not in TWICE], [0, 1])
 
         recip = keep.tile([P, N_TILES * CHUNKS, CHUNK], F32, name="recip")

@@ -28,25 +28,24 @@ RUN = 4
 ALIGN = 64
 
 TAB_ROW = P - 16
-UNITS = [(0, 0), (0, 1), (1, 0), (2, 0), (1, 1), (2, 1)]
+UNITS = [(0, 0), (0, 1), (1, 0), (1, 1), (2, 0), (2, 1)]
 HELD = {
     (0, 0, 0): "listed2",
-    (0, 0, 1): "plane_d",
-    (0, 0, 2): "w_bf0",
     (0, 0, 3): "v_words1",
     (0, 1, 0): "d_codes",
     (0, 1, 2): "staged2",
     (1, 0, 0): "v_words2",
+    (1, 0, 1): "w_raw11",
     (1, 0, 2): "e_bf00",
     (2, 0, 3): "w_words0",
-    (3, 0, 0): "bn_sb",
+    (3, 0, 0): "w_raw2",
+    (3, 0, 1): "bn_sb",
     (3, 0, 3): "w_words1",
-    (4, 0, 2): "e_words20",
-    (4, 0, 3): "e_words01",
-    (5, 0, 0): "e_bf11",
-    (5, 0, 1): "w_bf2",
+    (5, 0, 2): "e_bf11",
+    (5, 0, 3): "e_words01",
 }
-TWICE = ((0, 0),)
+TAKES = {"w_bf2": "e_bf01", "e_bf21": "e_bf11", "e_bf21_late": "w_raw2"}
+TWICE = ()
 ODD = 63
 
 
@@ -62,7 +61,7 @@ def tile_list_replay_kernel_control_kernel(
             return psum.tile([P, CHUNK], F32, name="bank%d" % b, tag="bank%d" % b)
 
         def tagged(tag, shape, dtype, name=None):
-            return keep.tile(shape, dtype, name=name or tag, tag=tag, align_bytes=ALIGN)
+            return keep.tile(shape, dtype, name=name or tag, tag=TAKES.get(tag, tag), align_bytes=ALIGN)
 
         v_list = keep.tile([P, S // 16], U16, name="v_list")
         q_list = keep.tile([P, S2 // 16], U16, name="q_list")
@@ -139,11 +138,16 @@ def tile_list_replay_kernel_control_kernel(
                 dst.rearrange("p (c i) t -> p c t i", i=RUN), src.rearrange("p t (c i) -> p c t i", i=RUN)
             )
 
-        def round_w_on_gpsimd(g):
+        def round_w_on_gpsimd(g, parts):
             w_bf[g] = tagged("w_bf%d" % g, [P, N, SLOTS], BF16)[:]
-            for ns in halves:
+            for ns in parts:
                 nc.gpsimd.tensor_scalar(
-                    w_bf[g][:, ns, :], w_raw[g, ns.start].rearrange("p t n -> p n t"), 1.0, 0.0, ALU.mult, ALU.add
+                    w_bf[g][:, ns, :].rearrange("p (c i) t -> p c t i", i=2),
+                    w_raw[g, ns.start].rearrange("p t (c i) -> p c t i", i=2),
+                    1.0,
+                    0.0,
+                    ALU.mult,
+                    ALU.add,
                 )
 
         def round_w(g):
@@ -175,9 +179,9 @@ def tile_list_replay_kernel_control_kernel(
                 nc.scalar.activation(e_rows[g, c][:, t, j], acc[:, j], ACT.Exp, bias=bias)
 
         def interleave_e(g, c, j=slice(0, CHUNK)):
-            if j.start == 0:
-                e_bf[g, c] = tagged("e_bf%d%d" % (g, c), [P, CHUNK, SLOTS], BF16)
-            interleave(e_bf[g, c][:, j, :], e_rows[g, c][:, :, j])
+            tag = "e_bf%d%d" % (g, c) + ("_late" if j.start else "")
+            e_bf[g, c, j.start] = tagged(tag, [P, j.stop - j.start, SLOTS], BF16)
+            interleave(e_bf[g, c, j.start][:], e_rows[g, c][:, :, j])
 
         def quantize_e(g, c, j=slice(0, CHUNK)):
             if j.start == 0:
@@ -185,7 +189,7 @@ def tile_list_replay_kernel_control_kernel(
             nc.vector.quantize_mx(
                 out=e_words[g, c][:, j].bitcast(FP8X4),
                 scales=e_scales[g, c][:, j],
-                in_=e_bf[g, c][:, j, :].rearrange("p j t -> p (j t)"),
+                in_=e_bf[g, c, j.start][:].rearrange("p j t -> p (j t)"),
             )
 
         listed = gather_v_scales(0, 2)
@@ -199,13 +203,11 @@ def tile_list_replay_kernel_control_kernel(
         nc.vector.tensor_copy(staged[:, 2 * PASS :].bitcast(U32), q_scales[:].bitcast(U32))
         move_rows(nc.sync, plane_first, staged[:])
         w_early = tagged("q_scales", [P, 3, SLOTS, N // 2], F32, "w_early")
-        load_w(0, halves[0], w_early[:, 0])
-        load_w(0, halves[1], w_early[:, 1])
-        load_w(1, halves[0], w_early[:, 2])
+        for k in range(3):
+            load_w(k // 2, halves[k % 2], w_early[:, k])
         first_bytes = plane_first[:].bitcast(U8)
         v_plane[0], v_plane[1] = first_bytes[:, :PASS], first_bytes[:, PASS : 2 * PASS]
         q_plane[0], q_plane[1] = first_bytes[:, 2 * PASS : 2 * PASS + CHUNK], first_bytes[:, 2 * PASS + CHUNK :]
-        load_w(1, halves[1], tagged("staged", [P, SLOTS, N // 2], F32, "w_raw11")[:])
         gather_v_words(0)
         gather_q_words(0, halves)
         gather_q_words(1, [slice(0, CHUNK)])
@@ -213,7 +215,7 @@ def tile_list_replay_kernel_control_kernel(
         kernel_values(0, 4, 1, halves[1])
         listed2 = gather_v_scales(2, 3)
         gather_v_words(1)
-        plane_d = tagged("plane_d", [P, PASSES * N // 4], I32)
+        plane_d = tagged("listed0", [P, PASSES * N // 4], I32, "plane_d")
         nc.gpsimd.memset(plane_d[:], 0)
         for r in range(4):
             nc.sync.dma_start(
@@ -231,17 +233,18 @@ def tile_list_replay_kernel_control_kernel(
             )
         move_rows(nc.sync, plane_v2, staged2[:])
         v_plane[2] = plane_v2[:].bitcast(U8)
-        load_w(2, slice(0, N), tagged("listed2", [P, SLOTS, N], F32, "w_raw2")[:])
         gather_v_words(2)
-        round_w_on_gpsimd(0)
-        round_w_on_gpsimd(1)
+        round_w_on_gpsimd(0, halves)
+        round_w_on_gpsimd(1, halves[:1])
         kernel_values(1, 0)
+        load_w(1, halves[1], tagged("w_raw11", [P, SLOTS, N // 2], F32)[:])
         kernel_values(2, 4)
-        kernel_values(3, 0)
+        kernel_values(3, 4)
+        load_w(2, slice(0, N), tagged("w_raw2", [P, SLOTS, N], F32)[:])
         bn_sb = tagged("bn_sb", [P, N_TILES], F32)
         with nc.allow_non_contiguous_dma(reason="one bias value a partition and row tile"):
             nc.sync.dma_start(bn_sb[:], bn.rearrange("(n p) -> p n", p=P))
-        kernel_values(4, 4)
+        kernel_values(4, 0)
         kernel_values(5, 4)
 
         def den_passes(c, tiles, passes):
@@ -281,35 +284,38 @@ def tile_list_replay_kernel_control_kernel(
         interleave_e(0, 0)
         interleave_e(0, 1)
         quantize_e(0, 0)
+        interleave(w_bf[1][:, halves[1], :], w_raw[1, halves[1].start])
         interleave_e(1, 0)
         quantize_w(0)
         quantize_e(1, 0)
-        interleave_e(2, 0)
         quantize_w(1)
-        quantize_e(2, 0)
+        for j in halves:
+            interleave_e(2, 0, j)
+        for j in halves:
+            quantize_e(2, 0, j)
         den_passes(0, range(N_TILES), [0, 1, 2])
         den_squares = keep.tile([P, N_TILES, CHUNK], F32, name="den_squares", tag="den_squares")
         for n in range(N_TILES):
             scratch[n, 0] = den_squares[:, n, :]
             if (n, 0) not in TWICE:
                 square_den(n, 0)
-        quantize_e(0, 1)
         interleave_e(1, 1)
-        round_w(2)
+        quantize_e(0, 1)
         quantize_e(1, 1)
+        round_w(2)
         interleave_e(2, 1, halves[0])
         quantize_w(2)
         interleave_e(2, 1, halves[1])
-        quantize_e(2, 1, halves[0])
-        quantize_e(2, 1, halves[1])
+        for j in halves:
+            quantize_e(2, 1, j)
         num_passes(0, range(N_TILES), [0, 1, 2])
         den_passes(1, [n for n in range(N_TILES) if (n, 0) not in TWICE], [0, 1])
 
         recip = keep.tile([P, N_TILES * CHUNKS, CHUNK], F32, name="recip")
         ratios, cut = {}, {}
+        ratio_first = tagged("w_bf2", [P, N_TILES, CHUNK], F32, "ratio_first")
 
-        def inverse(n, c, fine=False):
-            cuts = (0, CHUNK // 2, 3 * CHUNK // 4, CHUNK) if fine else (0, CHUNK)
+        def inverse(n, c, cuts=(0, CHUNK)):
             cut[n, c] = [slice(j0, j1) for j0, j1 in zip(cuts, cuts[1:])]
             for j in cut[n, c]:
                 if (n, c) in TWICE:
@@ -319,11 +325,11 @@ def tile_list_replay_kernel_control_kernel(
 
         def divide(n, c):
             r = scratch[n, c] if (n, c) in TWICE else recip[:, c * N_TILES + n, :]
-            ratio = keep.tile([P, CHUNK], F32, name="ratio%d%d" % (n, c))
+            ratio = ratio_first[:, n] if c == 0 else keep.tile([P, CHUNK], F32, name="ratio%d" % n)[:]
             for j in cut[n, c]:
                 nc.vector.tensor_tensor(ratio[:, j], num[n, c][:, j], r[:, j], ALU.mult)
             if (n, c) in TWICE:
-                nc.vector.tensor_tensor(recip[:, c * N_TILES + n, :], ratio[:], r, ALU.mult)
+                nc.vector.tensor_tensor(recip[:, c * N_TILES + n, :], ratio, r, ALU.mult)
                 ratio = recip[:, c * N_TILES + n, :]
             ratios[n, c] = ratio
 
@@ -338,10 +344,10 @@ def tile_list_replay_kernel_control_kernel(
                     adder.tensor_scalar(res[:, j], ratios[n, c][:, j], 1.0, bias, ALU.mult, ALU.add)
                 nc.sync.dma_start(out[n * P : (n + 1) * P, c * CHUNK + j.start : c * CHUNK + j.stop], res[:, j])
 
-        def finish(n, c):
+        def finish(n, c, engine):
             inverse(n, c)
             divide(n, c)
-            add_bias_and_store(n, c, "gpsimd")
+            add_bias_and_store(n, c, engine)
 
         for n in range(N_TILES):
             inverse(n, 0)
@@ -354,13 +360,13 @@ def tile_list_replay_kernel_control_kernel(
         for n in (0, 1):
             if (n, 1) not in TWICE:
                 square_den(n, 1)
-        finish(0, 1)
-        finish(1, 1)
+        finish(0, 1, "gpsimd")
+        finish(1, 1, "vector")
         square_den(2, 1)
         square_den(3, 1)
-        inverse(2, 1)
+        inverse(2, 1, (0, CHUNK // 2, CHUNK))
         divide(2, 1)
-        inverse(3, 1, True)
-        add_bias_and_store(2, 1, "scalar")
+        inverse(3, 1, (0, CHUNK // 2, 3 * CHUNK // 4, CHUNK))
+        add_bias_and_store(2, 1, "vector")
         divide(3, 1)
-        add_bias_and_store(3, 1, "vector")
+        add_bias_and_store(3, 1, "scalar")

@@ -25,7 +25,7 @@ CHUNKS = S2 // CHUNK
 N_TILES = N // P
 LIST_COLS = PASS // 16
 RUN = 4
-ALIGN = 64
+ALIGN = 256
 
 TAB_ROW = P - 16
 UNITS = [(0, 0), (0, 1), (1, 0), (1, 1), (2, 0), (2, 1)]

@@ -31,9 +31,9 @@ TAB_ROW = P - 16
 UNITS = [(0, 0), (0, 1), (1, 0), (1, 1), (2, 0), (2, 1)]
 HELD = {
     (0, 0, 0): "listed2",
-    (0, 0, 3): "v_words1",
-    (0, 1, 0): "d_codes",
-    (0, 1, 2): "staged2",
+    (0, 1, 3): "v_words1",
+    (0, 2, 0): "d_codes",
+    (0, 2, 2): "staged2",
     (1, 0, 0): "v_words2",
     (1, 0, 1): "w_raw11",
     (1, 0, 2): "e_bf00",
@@ -102,6 +102,8 @@ def tile_list_replay_kernel_control_kernel(
         w_scales = [tagged("w_scales%d" % g, [P, N], U8) for g in range(PASSES)]
         scratch = {(n, 1): keep.tile([P, CHUNK], F32, name="scratch%d" % n)[:] for n in range(N_TILES)}
         halves = [slice(0, CHUNK // 2), slice(CHUNK // 2, CHUNK)]
+
+        first_parts = [slice(0, CHUNK // 4), slice(CHUNK // 4, CHUNK // 2), halves[1]]
 
         def entries(k0, k1):
             return slice(k0 // 16, k1 // 16)
@@ -209,10 +211,10 @@ def tile_list_replay_kernel_control_kernel(
         v_plane[0], v_plane[1] = first_bytes[:, :PASS], first_bytes[:, PASS : 2 * PASS]
         q_plane[0], q_plane[1] = first_bytes[:, 2 * PASS : 2 * PASS + CHUNK], first_bytes[:, 2 * PASS + CHUNK :]
         gather_v_words(0)
-        gather_q_words(0, halves)
+        gather_q_words(0, first_parts)
         gather_q_words(1, [slice(0, CHUNK)])
-        kernel_values(0, 0, 0, halves[0])
-        kernel_values(0, 4, 1, halves[1])
+        for part, j in enumerate(first_parts):
+            kernel_values(0, SLOTS * (part % 2), part, j)
         listed2 = gather_v_scales(2, 3)
         gather_v_words(1)
         plane_d = tagged("listed0", [P, PASSES * N // 4], I32, "plane_d")
@@ -236,9 +238,9 @@ def tile_list_replay_kernel_control_kernel(
         gather_v_words(2)
         round_w_on_gpsimd(0, halves)
         round_w_on_gpsimd(1, halves[:1])
-        kernel_values(1, 0)
+        kernel_values(1, 4)
         load_w(1, halves[1], tagged("w_raw11", [P, SLOTS, N // 2], F32)[:])
-        kernel_values(2, 4)
+        kernel_values(2, 0)
         kernel_values(3, 4)
         load_w(2, slice(0, N), tagged("w_raw2", [P, SLOTS, N], F32)[:])
         bn_sb = tagged("bn_sb", [P, N_TILES], F32)
@@ -333,10 +335,11 @@ def tile_list_replay_kernel_control_kernel(
                 ratio = recip[:, c * N_TILES + n, :]
             ratios[n, c] = ratio
 
-        def add_bias_and_store(n, c, engine):
+        def add_bias_and_store(n, c, *engines):
             res = keep.tile([P, CHUNK], F32, name="res%d%d" % (n, c))
             bias = bn_sb[:, n : n + 1]
-            for j in cut[n, c]:
+            for k, j in enumerate(cut[n, c]):
+                engine = engines[k % len(engines)]
                 if engine == "scalar":
                     nc.scalar.activation(res[:, j], ratios[n, c][:, j], ACT.Identity, bias=bias)
                 else:
@@ -367,6 +370,6 @@ def tile_list_replay_kernel_control_kernel(
         inverse(2, 1, (0, CHUNK // 2, CHUNK))
         divide(2, 1)
         inverse(3, 1, (0, CHUNK // 2, 3 * CHUNK // 4, CHUNK))
-        add_bias_and_store(2, 1, "vector")
+        add_bias_and_store(2, 1, "gpsimd", "vector")
         divide(3, 1)
         add_bias_and_store(3, 1, "scalar")

@@ -24,7 +24,7 @@ CHUNK = 512
 CHUNKS = S2 // CHUNK
 N_TILES = N // P
 LIST_COLS = PASS // 16
-RUN = 4
+RUN = 8
 ALIGN = 256
 
 TAB_ROW = P - 16

from contextlib import ExitStack

import concourse.mybir as mybir

K, T, S, T2, S2, N = 512, 4096, 1536, 2048, 1024, 512
FLOPS = 2 * K * S * S2 + 2 * 2 * S * N * S2

F32 = mybir.dt.float32
BF16 = mybir.dt.bfloat16
I32 = mybir.dt.int32
U32 = mybir.dt.uint32
U16 = mybir.dt.uint16
U8 = mybir.dt.uint8
FP8X4 = mybir.dt.float8_e4m3fn_x4
FP4X4 = mybir.dt.float4_e2m1fn_x4
ACT = mybir.ActivationFunctionType
ALU = mybir.AluOpType

P = 128
SLOTS = 4
PASS = P * SLOTS
PASSES = S // PASS
CHUNK = 512
CHUNKS = S2 // CHUNK
N_TILES = N // P
LIST_COLS = PASS // 16
RUN = 8
ALIGN = 256

TAB_ROW = P - 16
UNITS = [(0, 0), (0, 1), (1, 0), (1, 1), (2, 0), (2, 1)]
HELD = {
    (0, 0, 0): "listed2",
    (0, 1, 3): "v_words1",
    (0, 2, 0): "d_codes",
    (0, 2, 2): "staged2",
    (1, 0, 0): "v_words2",
    (1, 0, 1): "w_raw11",
    (1, 0, 2): "e_bf00",
    (2, 0, 3): "w_words0",
    (3, 0, 0): "w_raw2",
    (3, 0, 1): "bn_sb",
    (3, 0, 3): "w_words1",
    (5, 0, 2): "e_bf11",
    (5, 0, 3): "e_words01",
}
TAKES = {"w_bf2": "e_bf01", "e_bf21": "e_bf11", "e_bf21_late": "w_raw2"}
TWICE = ()
ODD = 63


def tile_list_replay_kernel_control_kernel(
    tc, tab_words, tab_scales, tab2_words, tab2_scales, offs, offs2, wg, w, d_words, d_scales, bn, out
):
    nc = tc.nc
    with ExitStack() as ctx:
        keep = ctx.enter_context(tc.tile_pool(name="keep", bufs=1))
        psum = ctx.enter_context(tc.psum_pool(name="psum", bufs=1))

        def bank(b):
            return psum.tile([P, CHUNK], F32, name="bank%d" % b, tag="bank%d" % b)

        def tagged(tag, shape, dtype, name=None):
            return keep.tile(shape, dtype, name=name or tag, tag=TAKES.get(tag, tag), align_bytes=ALIGN)

        v_list = keep.tile([P, S // 16], U16, name="v_list")
        q_list = keep.tile([P, S2 // 16], U16, name="q_list")
        v_tab_scales = tagged("v_tab_scales", [P, T // 4], I32)
        q_tab_scales = tagged("q_tab_scales", [P, T2 // 4], I32)
        v_tab_words = keep.tile([P, T], I32, name="v_tab_words")
        q_tab_words = keep.tile([P, T2], I32, name="q_tab_words")
        wg_sb = keep.tile([P, PASSES, SLOTS], F32, name="wg_sb")
        ln_wg = keep.tile([P, PASSES * SLOTS], F32, name="ln_wg", tag="den_squares")
        held_bias = {key: tagged(tag, [P, 1], F32, "bias_" + tag) for key, tag in HELD.items()}
        warm = keep.tile([P, 1], F32, name="warm")

        nc.vector.memset(v_tab_scales[0:TAB_ROW], 0)
        nc.vector.memset(q_tab_scales[0:TAB_ROW], 0)
        plane_first = tagged("plane_first", [P, (2 * PASS + S2) // 4], I32)
        plane_v2 = tagged("plane_v2", [P, PASS // 4], I32)
        nc.gpsimd.memset(plane_first[:], 0)
        nc.gpsimd.memset(plane_v2[:], 0)

        nc.sync.dma_start(v_list[:], offs)
        nc.scalar.dma_start(v_tab_scales[TAB_ROW:P], tab_scales[0].bitcast(I32))
        nc.sync.dma_start(q_list[:], offs2)
        nc.scalar.dma_start(q_tab_scales[TAB_ROW:P], tab2_scales[0].bitcast(I32))
        nc.sync.dma_start(v_tab_words[:], tab_words[0].rearrange("p t i -> p (t i)").bitcast(I32))
        nc.scalar.dma_start(wg_sb[:], wg.rearrange("(g p t) -> p g t", p=P, t=SLOTS))
        nc.sync.dma_start(q_tab_words[:], tab2_words[0].rearrange("p t i -> p (t i)").bitcast(I32))

        nc.scalar.activation(ln_wg[:], wg_sb[:].rearrange("p g t -> p (g t)"), ACT.Ln)
        for (u, half, t), tile in held_bias.items():
            col = UNITS[u][0] * SLOTS + t
            nc.scalar.copy(tile[:], ln_wg[:, col : col + 1])
        nc.scalar.activation(warm[:], ln_wg[:, 0:1], ACT.Exp)

        q_words, v_words, w_raw, e_bf, den, num = {}, {}, {}, {}, {}, {}
        e_words, w_words, w_bf, v_plane, q_plane = {}, {}, {}, {}, {}
        e_scales = {u: tagged("e_scales%d%d" % u, [P, CHUNK], U8) for u in UNITS}
        e_rows = {u: tagged("e_rows%d%d" % u, [P, SLOTS, CHUNK], BF16) for u in UNITS}
        w_scales = [tagged("w_scales%d" % g, [P, N], U8) for g in range(PASSES)]
        scratch = {(n, 1): keep.tile([P, CHUNK], F32, name="scratch%d" % n)[:] for n in range(N_TILES)}
        halves = [slice(0, CHUNK // 2), slice(CHUNK // 2, CHUNK)]

        first_parts = [slice(0, CHUNK // 4), slice(CHUNK // 4, CHUNK // 2), halves[1]]

        def entries(k0, k1):
            return slice(k0 // 16, k1 // 16)

        def gather_q_words(c, parts):
            q_words[c] = tagged("q_words%d" % c, [P, CHUNK], U32)
            for j in parts:
                cols = entries(c * CHUNK + j.start, c * CHUNK + j.stop)
                nc.vector.tensor_copy(q_words[c][:, j], q_tab_words[:].bitcast(U32).indirect(q_list[:, cols]))

        def gather_v_scales(g0, g1):
            listed = tagged("listed%d" % g0, [P, (g1 - g0) * PASS], U8)
            cols = entries(g0 * PASS, g1 * PASS)
            nc.vector.tensor_copy(listed[:], v_tab_scales[:].bitcast(U8).indirect(v_list[:, cols]))
            return listed

        def gather_v_words(g):
            v_words[g] = tagged("v_words%d" % g, [P, PASS], U32)
            nc.vector.tensor_copy(
                v_words[g][:].rearrange("p (t m) -> p m t", t=SLOTS),
                v_tab_words[:].bitcast(U32).indirect(v_list[:, entries(g * PASS, (g + 1) * PASS)]),
            )

        def move_rows(queue, plane, rows):
            for r in range(4):
                queue.dma_start(plane[r:P:32], rows[TAB_ROW + r : P : 4].bitcast(I32))

        def load_w(g, ns, dst):
            w_raw[g, ns.start] = dst
            nc.sync.dma_start(dst, w[g * PASS : (g + 1) * PASS, ns].rearrange("(p t) n -> p t n", t=SLOTS))

        def interleave(dst, src):
            nc.vector.tensor_copy(
                dst.rearrange("p (c i) t -> p c t i", i=RUN), src.rearrange("p t (c i) -> p c t i", i=RUN)
            )

        def round_w_on_gpsimd(g, parts):
            w_bf[g] = tagged("w_bf%d" % g, [P, N, SLOTS], BF16)[:]
            for ns in parts:
                nc.gpsimd.tensor_scalar(
                    w_bf[g][:, ns, :].rearrange("p (c i) t -> p c t i", i=2),
                    w_raw[g, ns.start].rearrange("p t (c i) -> p c t i", i=2),
                    1.0,
                    0.0,
                    ALU.mult,
                    ALU.add,
                )

        def round_w(g):
            w_bf[g] = tagged("w_bf%d" % g, [P, N, SLOTS], BF16)[:]
            interleave(w_bf[g], w_raw[g, 0])

        def quantize_w(g):
            w_words[g] = tagged("w_words%d" % g, [P, N], U32)
            nc.vector.quantize_mx(
                out=w_words[g][:].bitcast(FP8X4), scales=w_scales[g][:], in_=w_bf[g].rearrange("p n t -> p (n t)")
            )

        def kernel_values(u, first_bank, half=0, j=slice(0, CHUNK)):
            g, c = UNITS[u]
            for t in range(SLOTS):
                acc = bank(first_bank + t)
                m = slice(t * P, (t + 1) * P)
                nc.tensor.matmul_mx(
                    out=acc[:, j],
                    lhsT=v_words[g][:, m].bitcast(FP8X4),
                    lhsT_scale=v_plane[g][:, m],
                    rhs=q_words[c][:, j].bitcast(FP8X4),
                    rhs_scale=q_plane[c][:, j],
                    start=True,
                    stop=True,
                )
                col = g * SLOTS + t
                bias = held_bias[u, half, t][:] if (u, half, t) in held_bias else ln_wg[:, col : col + 1]
                nc.scalar.activation(e_rows[g, c][:, t, j], acc[:, j], ACT.Exp, bias=bias)

        def interleave_e(g, c, j=slice(0, CHUNK)):
            tag = "e_bf%d%d" % (g, c) + ("_late" if j.start else "")
            e_bf[g, c, j.start] = tagged(tag, [P, j.stop - j.start, SLOTS], BF16)
            interleave(e_bf[g, c, j.start][:], e_rows[g, c][:, :, j])

        def quantize_e(g, c, j=slice(0, CHUNK)):
            if j.start == 0:
                e_words[g, c] = tagged("e_words%d%d" % (g, c), [P, CHUNK], U32)
            nc.vector.quantize_mx(
                out=e_words[g, c][:, j].bitcast(FP8X4),
                scales=e_scales[g, c][:, j],
                in_=e_bf[g, c, j.start][:].rearrange("p j t -> p (j t)"),
            )

        listed = gather_v_scales(0, 2)
        q_scales = tagged("q_scales", [P, S2], U8)
        nc.vector.tensor_copy(q_scales[:], q_tab_scales[:].bitcast(U8).indirect(q_list[:]))
        staged = tagged("staged", [P, 2 * PASS + S2], U8)
        nc.vector.tensor_copy(
            staged[:, : 2 * PASS].rearrange("p (g t m) -> p t g m", t=SLOTS, m=P),
            listed[:].rearrange("p (g m t) -> p t g m", t=SLOTS, m=P),
        )
        nc.vector.tensor_copy(staged[:, 2 * PASS :].bitcast(U32), q_scales[:].bitcast(U32))
        move_rows(nc.sync, plane_first, staged[:])
        w_early = tagged("q_scales", [P, 3, SLOTS, N // 2], F32, "w_early")
        for k in range(3):
            load_w(k // 2, halves[k % 2], w_early[:, k])
        first_bytes = plane_first[:].bitcast(U8)
        v_plane[0], v_plane[1] = first_bytes[:, :PASS], first_bytes[:, PASS : 2 * PASS]
        q_plane[0], q_plane[1] = first_bytes[:, 2 * PASS : 2 * PASS + CHUNK], first_bytes[:, 2 * PASS + CHUNK :]
        gather_v_words(0)
        gather_q_words(0, first_parts)
        gather_q_words(1, [slice(0, CHUNK)])
        for part, j in enumerate(first_parts):
            kernel_values(0, SLOTS * (part % 2), part, j)
        listed2 = gather_v_scales(2, 3)
        gather_v_words(1)
        plane_d = tagged("listed0", [P, PASSES * N // 4], I32, "plane_d")
        nc.gpsimd.memset(plane_d[:], 0)
        for r in range(4):
            nc.sync.dma_start(
                plane_d[r:P:32].rearrange("q (g n) -> q g n", g=PASSES),
                d_scales.rearrange("g r n -> r g n")[r:16:4].bitcast(I32),
            )
        d_plane = plane_d[:].bitcast(U8)
        d_codes = tagged("d_codes", [P, PASSES, 2 * N // 4], I32)
        nc.sync.dma_start(d_codes[:], d_words.rearrange("g p b -> p g b").bitcast(I32))
        staged2 = tagged("staged2", [P, PASS], U8)
        for m in (slice(0, ODD), slice(ODD, P)):
            nc.vector.tensor_copy(
                staged2[:].rearrange("p (t m) -> p m t", t=SLOTS)[:, m, :],
                listed2[:].rearrange("p (m t) -> p m t", t=SLOTS)[:, m, :],
            )
        move_rows(nc.sync, plane_v2, staged2[:])
        v_plane[2] = plane_v2[:].bitcast(U8)
        gather_v_words(2)
        round_w_on_gpsimd(0, halves)
        round_w_on_gpsimd(1, halves[:1])
        kernel_values(1, 4)
        load_w(1, halves[1], tagged("w_raw11", [P, SLOTS, N // 2], F32)[:])
        kernel_values(2, 0)
        kernel_values(3, 4)
        load_w(2, slice(0, N), tagged("w_raw2", [P, SLOTS, N], F32)[:])
        bn_sb = tagged("bn_sb", [P, N_TILES], F32)
        with nc.allow_non_contiguous_dma(reason="one bias value a partition and row tile"):
            nc.sync.dma_start(bn_sb[:], bn.rearrange("(n p) -> p n", p=P))
        kernel_values(4, 0)
        kernel_values(5, 4)

        def den_passes(c, tiles, passes):
            for g in passes:
                for n in tiles:
                    if g == 0:
                        den[n, c] = bank(n)
                    nc.tensor.matmul_mx(
                        out=den[n, c][:],
                        lhsT=d_codes[:, g, n * 2 * P // 4 : (n + 1) * 2 * P // 4].bitcast(U8).bitcast(FP4X4),
                        lhsT_scale=d_plane[:, g * N + n * P : g * N + (n + 1) * P],
                        rhs=e_words[g, c][:].bitcast(FP8X4),
                        rhs_scale=e_scales[g, c][:],
                        start=(g == 0),
                        stop=(g == PASSES - 1),
                    )

        def num_passes(c, tiles, passes):
            for g in passes:
                for n in tiles:
                    if g == 0:
                        num[n, c] = bank(N_TILES + n)
                    m = slice(n * P, (n + 1) * P)
                    nc.tensor.matmul_mx(
                        out=num[n, c][:],
                        lhsT=w_words[g][:, m].bitcast(FP8X4),
                        lhsT_scale=w_scales[g][:, m],
                        rhs=e_words[g, c][:].bitcast(FP8X4),
                        rhs_scale=e_scales[g, c][:],
                        start=(g == 0),
                        stop=(g == PASSES - 1),
                    )

        def square_den(n, c):
            nc.scalar.activation(scratch[n, c], den[n, c][:], ACT.Square)

        interleave_e(0, 0)
        interleave_e(0, 1)
        quantize_e(0, 0)
        interleave(w_bf[1][:, halves[1], :], w_raw[1, halves[1].start])
        interleave_e(1, 0)
        quantize_w(0)
        quantize_e(1, 0)
        quantize_w(1)
        for j in halves:
            interleave_e(2, 0, j)
        for j in halves:
            quantize_e(2, 0, j)
        den_passes(0, range(N_TILES), [0, 1, 2])
        den_squares = keep.tile([P, N_TILES, CHUNK], F32, name="den_squares", tag="den_squares")
        for n in range(N_TILES):
            scratch[n, 0] = den_squares[:, n, :]
            if (n, 0) not in TWICE:
                square_den(n, 0)
        interleave_e(1, 1)
        quantize_e(0, 1)
        quantize_e(1, 1)
        round_w(2)
        interleave_e(2, 1, halves[0])
        quantize_w(2)
        interleave_e(2, 1, halves[1])
        for j in halves:
            quantize_e(2, 1, j)
        num_passes(0, range(N_TILES), [0, 1, 2])
        den_passes(1, [n for n in range(N_TILES) if (n, 0) not in TWICE], [0, 1])

        recip = keep.tile([P, N_TILES * CHUNKS, CHUNK], F32, name="recip")
        ratios, cut = {}, {}
        ratio_first = tagged("w_bf2", [P, N_TILES, CHUNK], F32, "ratio_first")

        def inverse(n, c, cuts=(0, CHUNK)):
            cut[n, c] = [slice(j0, j1) for j0, j1 in zip(cuts, cuts[1:])]
            for j in cut[n, c]:
                if (n, c) in TWICE:
                    nc.scalar.activation(scratch[n, c][:, j], den[n, c][:, j], ACT.Abs_reciprocal_sqrt)
                else:
                    nc.scalar.activation(recip[:, c * N_TILES + n, j], scratch[n, c][:, j], ACT.Abs_reciprocal_sqrt)

        def divide(n, c):
            r = scratch[n, c] if (n, c) in TWICE else recip[:, c * N_TILES + n, :]
            ratio = ratio_first[:, n] if c == 0 else keep.tile([P, CHUNK], F32, name="ratio%d" % n)[:]
            for j in cut[n, c]:
                nc.vector.tensor_tensor(ratio[:, j], num[n, c][:, j], r[:, j], ALU.mult)
            if (n, c) in TWICE:
                nc.vector.tensor_tensor(recip[:, c * N_TILES + n, :], ratio, r, ALU.mult)
                ratio = recip[:, c * N_TILES + n, :]
            ratios[n, c] = ratio

        def add_bias_and_store(n, c, *engines):
            res = keep.tile([P, CHUNK], F32, name="res%d%d" % (n, c))
            bias = bn_sb[:, n : n + 1]
            for k, j in enumerate(cut[n, c]):
                engine = engines[k % len(engines)]
                if engine == "scalar":
                    nc.scalar.activation(res[:, j], ratios[n, c][:, j], ACT.Identity, bias=bias)
                else:
                    adder = nc.vector if engine == "vector" else nc.gpsimd
                    adder.tensor_scalar(res[:, j], ratios[n, c][:, j], 1.0, bias, ALU.mult, ALU.add)
                nc.sync.dma_start(out[n * P : (n + 1) * P, c * CHUNK + j.start : c * CHUNK + j.stop], res[:, j])

        def finish(n, c, engine):
            inverse(n, c)
            divide(n, c)
            add_bias_and_store(n, c, engine)

        for n in range(N_TILES):
            inverse(n, 0)
        den_passes(1, [n for n in range(N_TILES) if (n, 0) in TWICE], [0, 1])
        den_passes(1, range(N_TILES), [2])
        for n in range(N_TILES):
            divide(n, 0)
            add_bias_and_store(n, 0, "gpsimd")
            num_passes(1, [n], [0, 1, 2])
        for n in (0, 1):
            if (n, 1) not in TWICE:
                square_den(n, 1)
        finish(0, 1, "gpsimd")
        finish(1, 1, "vector")
        square_den(2, 1)
        square_den(3, 1)
        inverse(2, 1, (0, CHUNK // 2, CHUNK))
        divide(2, 1)
        inverse(3, 1, (0, CHUNK // 2, 3 * CHUNK // 4, CHUNK))
        add_bias_and_store(2, 1, "gpsimd", "vector")
        divide(3, 1)
        add_bias_and_store(3, 1, "scalar")
